import numpy as np
import ml_dtypes


def mxq(x, axis, fmt="e4m3"):
    dtype, down = {"e4m3": (ml_dtypes.float8_e4m3fn, 7), "e5m2": (ml_dtypes.float8_e5m2, 14)}[fmt]
    v = np.moveaxis(np.asarray(x, np.float32).astype(ml_dtypes.bfloat16).astype(np.float64), axis, -1)
    blocks = v.reshape(v.shape[:-1] + (-1, 32))
    amax = np.abs(blocks).max(-1, keepdims=True)
    byte = np.maximum(np.where(amax > 0, np.frexp(amax)[1] - 1 + 127, 0) - down, 1)
    scale = np.exp2(byte - 127.0)
    codes = (blocks / scale).astype(np.float32).astype(dtype).astype(np.float64)
    return np.moveaxis((codes * scale).reshape(v.shape), -1, axis)


WIDE = False


def mx_kscale(k):
    if not WIDE:
        return np.ones(k)
    levels = np.array([10, -10, 5, -5, 0])
    if k % 512:
        return np.exp2(np.random.permutation(np.resize(levels, k // 32))).repeat(32)
    a = np.empty((k // 512, 16))
    for p in range(k // 512):
        a[p, :8] = np.random.permutation(np.resize(levels, 8))
        for g in range(8):
            far = levels[np.abs(levels - a[p, g]) >= 10]
            a[p, g + 8] = far[np.random.randint(len(far))]
    return np.exp2(a.ravel()).repeat(32)


def f64(x):
    return np.asarray(x).astype(np.float64)


def striped(idx):
    return np.tile(np.asarray(idx).reshape(-1, 16).T, (8, 1)).astype(np.uint16)


def unstriped(offs):
    return offs[:16].T.reshape(-1).astype(np.int64)


def bf(x):
    return np.asarray(x, np.float32).astype(ml_dtypes.bfloat16)


def planes(Y):
    r, m = Y.shape
    b = f64(bf(Y)).reshape(r // 32, 32, m)
    amax = np.abs(b).max(1)
    byte = np.clip(np.where(amax > 0, np.frexp(amax)[1] - 1 + 127 - 7, 1), 1, 254)
    codes = (b * np.exp2(127.0 - byte)[:, None, :]).reshape(r, m).astype(np.float32).astype(ml_dtypes.float8_e4m3fn).view(np.uint8)
    words = codes.reshape(r // 512, 128, 4, m).transpose(0, 1, 3, 2)
    return np.ascontiguousarray(words), np.ascontiguousarray(byte.astype(np.uint8).reshape(r // 512, 16, m))


D, T, I, G, M = 512, 2048, 1024, 128, 512


def setup_inputs():
    n = np.random.standard_normal
    idx = (np.random.permutation(T // 8)[:I // 8, None] * 8 + np.arange(8)).reshape(-1)
    fd = mx_kscale(D)
    return {
        "keys": (n((D, T)) / fd[:, None]).astype(np.float32),
        "imp": np.tile(np.random.uniform(0.2, 1.0, T), (128, 1)).astype(np.float32),
        "pf": (np.random.uniform(0.2, 0.6, (1, G))).astype(np.float32),
        "wd": (n((D, M)) * 1 / np.sqrt(D) * fd[:, None]).astype(np.float32),
        "offs": striped(idx),
    }


def reference(keys, imp, pf, wd, offs):
    idx = unstriped(offs)
    x = f64(keys)[:, idx] * f64(imp)[:1][:, idx]
    b = x.reshape(D, G, I // G).sum(axis=2) * f64(pf)
    wdq = mxq(f64(wd), 0, "e4m3")
    bq = mxq(b, 0, "e4m3")
    y = wdq.T @ bq
    words, scales = planes(y)
    return y, words, scales

@@ -1,0 +1,129 @@
+from contextlib import ExitStack
+
+import concourse.mybir as mybir
+from concourse.masks import make_identity
+
+D, T, I, G, M = 512, 2048, 1024, 128, 512
+FLOPS = 2 * D * M * G
+
+F32 = mybir.dt.float32
+BF16 = mybir.dt.bfloat16
+U32 = mybir.dt.uint32
+I32 = mybir.dt.int32
+U16 = mybir.dt.uint16
+U8 = mybir.dt.uint8
+FP8X4 = mybir.dt.float8_e4m3fn_x4
+MULT = mybir.AluOpType.mult
+ADD = mybir.AluOpType.add
+AXIS_X = mybir.AxisListType.X
+
+P = 128
+PACK = 4
+PAGE = I // G
+PE_PLANES = 2
+
+
+def tile_attend_pagesummary_pl_kernel(tc, keys, imp, pf, wd, offs, out_0, out_1, out_2):
+    nc = tc.nc
+    with ExitStack() as ctx:
+        sb = ctx.enter_context(tc.tile_pool(name="sb", bufs=1))
+        ps = ctx.enter_context(tc.psum_pool(name="ps", bufs=1))
+
+        offsets = sb.tile([P, I // 16], U16, name="offsets")
+        imp_cols = sb.tile([P, 2, 8], F32, name="imp_cols")
+        pf_col = sb.tile([P, 1], F32, name="pf_col")
+        nc.sync.dma_start(imp_cols[:], imp[0].rearrange("(h p c) -> p h c", h=2, c=8))
+        nc.scalar.dma_start(pf_col[:], pf.rearrange("o g -> g o"))
+        nc.sync.dma_start(offsets[:], offs)
+        key_rows = keys.rearrange("(p t) n -> t p n", t=PACK)
+        key_planes = []
+        for t in range(PACK):
+            plane = sb.tile([P, T], F32, name=f"keys{t}")
+            nc.sync.dma_start(plane[:], key_rows[t])
+            key_planes.append(plane)
+        wd_raw = []
+        for h in range(2):
+            raw = sb.tile([P, PACK, M // 2], F32, name=f"wd_raw{h}")
+            nc.sync.dma_start(raw[:], wd[:, h * 256:(h + 1) * 256].rearrange("(p j) m -> p j m", j=PACK))
+            wd_raw.append(raw)
+
+        ident = sb.tile([P, P], F32, name="ident")
+        make_identity(nc, ident[:])
+
+        pf_ps = ps.tile([P, G], F32, name="pf_ps", tag="bank4")
+        nc.tensor.transpose(pf_ps[:], pf_col[:].to_broadcast([P, P]), ident[:])
+        pf_slots = sb.tile([P, I], F32, name="pf_slots")
+        nc.vector.tensor_copy(pf_slots[:].rearrange("p (g j) -> p g j", j=PAGE),
+                              pf_ps[:].unsqueeze(2).to_broadcast([P, G, PAGE]))
+
+        imp_win = sb.tile([P, T], F32, name="imp_win")
+        imp_view = imp_win[:].rearrange("p (h n q c) -> p h q n c", h=2, q=2, c=4)
+        for q in range(2):
+            for h in (1, 0):
+                bank = ps.tile([P, 4, P], F32, name=f"imp_ps{h}{q}", tag=f"bank{2 * h + q}")
+                for c in range(4):
+                    nc.tensor.transpose(bank[:, c, :], imp_cols[:, h, 4 * q + c:4 * q + c + 1].to_broadcast([P, P]), ident[:])
+                if h == 0:
+                    nc.vector.tensor_copy(imp_view[:, h, q], bank[:].rearrange("p c n -> p n c"))
+                else:
+                    nc.scalar.copy(imp_view[:, h, q], bank[:].rearrange("p c n -> p n c"))
+
+        weight = sb.tile([P, I], F32, name="weight")
+        nc.vector.tensor_tensor(weight[:], imp_win[:].indirect(offsets[:]), pf_slots[:], MULT)
+
+        b_grp = sb.tile([P, G, PACK], BF16, name="b_grp", align_bytes=64)
+        back = ps.tile([P, PE_PLANES, G], F32, name="back", tag="bank7")
+        for t in range(PACK):
+            x = sb.tile([P, I], F32, name=f"x{t}")
+            nc.vector.tensor_tensor(x[:], key_planes[t][:].indirect(offsets[:]), weight[:], MULT)
+            x_pages = x[:].rearrange("p (g j) -> p g j", j=PAGE)
+            if t < PE_PLANES:
+                sums = ps.tile([P, P], F32, name=f"sums{t}", tag=f"bank{5 + t}")
+                for j in range(PAGE):
+                    nc.tensor.matmul(sums[:], x_pages[:, :, j], ident[:], start=(j == 0), stop=(j == PAGE - 1), is_transpose=True)
+                turned = sb.tile([P, P], F32, name=f"turned{t}")
+                nc.scalar.copy(turned[:], sums[:])
+                nc.tensor.transpose(back[:, t, :], turned[:], ident[:])
+                if t == PE_PLANES - 1:
+                    nc.scalar.copy(b_grp[:, :, 0:PE_PLANES], back[:].rearrange("p t g -> p g t"))
+            else:
+                with nc.allow_low_precision(reason="float32 sum, rounded once for the quantiser"):
+                    nc.vector.tensor_reduce(b_grp[:, :, t], x_pages, AXIS_X, ADD)
+
+        w_codes = sb.tile([P, PACK, P], U32, name="w_codes", align_bytes=64)
+        w_scales = sb.tile([P, PACK, P], U8, name="w_scales", align_bytes=64)
+        for h in range(2):
+            grp = sb.tile([P, PACK, 64, PACK], BF16, name=f"w_grp{h}", align_bytes=64)
+            nc.scalar.copy(grp[:].rearrange("p t s j -> p s j t"), wd_raw[h][:].rearrange("p j (s t) -> p s j t", t=PACK))
+            for t in range(PACK):
+                nc.vector.quantize_mx(out=w_codes[:, t, 64 * h:64 * h + 64].bitcast(FP8X4),
+                                      scales=w_scales[:, t, 64 * h:64 * h + 64],
+                                      in_=grp[:, t].rearrange("p s j -> p (s j)"))
+
+        b_codes = sb.tile([P, G], U32, name="b_codes", align_bytes=64)
+        b_scales = sb.tile([P, G], U8, name="b_scales", align_bytes=64)
+        nc.vector.quantize_mx(out=b_codes[:].bitcast(FP8X4), scales=b_scales[:], in_=b_grp[:].rearrange("p g t -> p (g t)"))
+
+        y = sb.tile([P, PACK, G], F32, name="y")
+        out_rows = out_0.rearrange("(p t) g -> p t g", t=PACK)
+        for u in range(2):
+            acc = ps.tile([P, 2, G], F32, name=f"acc{u}", tag=f"bank{u}")
+            for v in range(2):
+                t = 2 * u + v
+                nc.tensor.matmul_mx(out=acc[:, v, :], lhsT=w_codes[:, t, :].bitcast(FP8X4), lhsT_scale=w_scales[:, t, :],
+                                    rhs=b_codes[:].bitcast(FP8X4), rhs_scale=b_scales[:], start=True, stop=True)
+            if u == 0:
+                nc.scalar.copy(y[:, 0:2, :], acc[:])
+            else:
+                nc.vector.tensor_copy(y[:, 2:4, :], acc[:])
+        nc.sync.dma_start(out_rows, y[:])
+
+        y_grp = sb.tile([P, G, PACK], BF16, name="y_grp", align_bytes=64)
+        nc.vector.tensor_copy(y_grp[:].rearrange("p (c i) t -> p c t i", i=4), y[:].rearrange("p t (c i) -> p c t i", i=4))
+        y_codes = sb.tile([P, G], U32, name="y_codes", align_bytes=64)
+        y_scales = sb.tile([P, G], U8, name="y_scales", align_bytes=64)
+        nc.vector.quantize_mx(out=y_codes[:].bitcast(FP8X4), scales=y_scales[:], in_=y_grp[:].rearrange("p g t -> p (g t)"))
+        nc.sync.dma_start(out_1[0].rearrange("p c r -> p (c r)").bitcast(I32), y_codes[:].bitcast(I32))
+        for q in range(4):
+            queue = nc.sync if q < 2 else nc.scalar
+            queue.dma_start(out_2[0, 4 * q:4 * q + 4, :].bitcast(I32), y_scales[32 * q:32 * q + 4, :].bitcast(I32))

@@ -20,7 +20,7 @@ AXIS_X = mybir.AxisListType.X
 P = 128
 PACK = 4
 PAGE = I // G
-PE_PLANES = 2
+IMP_DMA = 1024
 
 
 def tile_attend_pagesummary_pl_kernel(tc, keys, imp, pf, wd, offs, out_0, out_1, out_2):
@@ -30,75 +30,88 @@ def tile_attend_pagesummary_pl_kernel(tc, keys, imp, pf, wd, offs, out_0, out_1,
         ps = ctx.enter_context(tc.psum_pool(name="ps", bufs=1))
 
         offsets = sb.tile([P, I // 16], U16, name="offsets")
-        imp_cols = sb.tile([P, 2, 8], F32, name="imp_cols")
+        imp_cols = sb.tile([P, 2, 4], F32, name="imp_cols")
+        imp_win = sb.tile([P, T], F32, name="imp_win")
         pf_col = sb.tile([P, 1], F32, name="pf_col")
-        nc.sync.dma_start(imp_cols[:], imp[0].rearrange("(h p c) -> p h c", h=2, c=8))
-        nc.scalar.dma_start(pf_col[:], pf.rearrange("o g -> g o"))
+        nc.sync.dma_start(pf_col[:], pf.rearrange("o g -> g o"))
+        nc.sync.dma_start(imp_cols[:], imp[0, IMP_DMA:T].rearrange("(q p c) -> p q c", q=2, c=4))
+        nc.sync.dma_start(imp_win[:, 0:IMP_DMA], imp[:, 0:IMP_DMA])
         nc.sync.dma_start(offsets[:], offs)
+        wd_raw = [sb.tile([P, PACK, M // 2], F32, name=f"wd_raw{h}", tag=f"wd_raw{h}") for h in range(2)]
+        wd_halves = [wd[:, h * 256:(h + 1) * 256].rearrange("(p j) m -> p j m", j=PACK) for h in range(2)]
+        nc.sync.dma_start(wd_raw[0][:], wd_halves[0])
         key_rows = keys.rearrange("(p t) n -> t p n", t=PACK)
         key_planes = []
         for t in range(PACK):
-            plane = sb.tile([P, T], F32, name=f"keys{t}")
+            plane = sb.tile([P, T], F32, name=f"keys{t}", tag=f"keys{t}")
             nc.sync.dma_start(plane[:], key_rows[t])
             key_planes.append(plane)
-        wd_raw = []
-        for h in range(2):
-            raw = sb.tile([P, PACK, M // 2], F32, name=f"wd_raw{h}")
-            nc.sync.dma_start(raw[:], wd[:, h * 256:(h + 1) * 256].rearrange("(p j) m -> p j m", j=PACK))
-            wd_raw.append(raw)
+        nc.sync.dma_start(wd_raw[1][:], wd_halves[1])
 
         ident = sb.tile([P, P], F32, name="ident")
         make_identity(nc, ident[:])
 
-        pf_ps = ps.tile([P, G], F32, name="pf_ps", tag="bank4")
+        pf_ps = ps.tile([P, G], F32, name="pf_ps", tag="bank2")
         nc.tensor.transpose(pf_ps[:], pf_col[:].to_broadcast([P, P]), ident[:])
-        pf_slots = sb.tile([P, I], F32, name="pf_slots")
+        pf_slots = sb.tile([P, I], F32, name="pf_slots", tag="pf_slots", align_bytes=64)
         nc.vector.tensor_copy(pf_slots[:].rearrange("p (g j) -> p g j", j=PAGE),
                               pf_ps[:].unsqueeze(2).to_broadcast([P, G, PAGE]))
 
-        imp_win = sb.tile([P, T], F32, name="imp_win")
-        imp_view = imp_win[:].rearrange("p (h n q c) -> p h q n c", h=2, q=2, c=4)
         for q in range(2):
-            for h in (1, 0):
-                bank = ps.tile([P, 4, P], F32, name=f"imp_ps{h}{q}", tag=f"bank{2 * h + q}")
-                for c in range(4):
-                    nc.tensor.transpose(bank[:, c, :], imp_cols[:, h, 4 * q + c:4 * q + c + 1].to_broadcast([P, P]), ident[:])
-                if h == 0:
-                    nc.vector.tensor_copy(imp_view[:, h, q], bank[:].rearrange("p c n -> p n c"))
-                else:
-                    nc.scalar.copy(imp_view[:, h, q], bank[:].rearrange("p c n -> p n c"))
+            imp_ps = ps.tile([P, 4, P], F32, name=f"imp_ps{q}", tag=f"bank{q}")
+            for c in range(4):
+                nc.tensor.transpose(imp_ps[:, c, :], imp_cols[:, q, c:c + 1].to_broadcast([P, P]), ident[:])
+            cols = slice(IMP_DMA + 512 * q, IMP_DMA + 512 * (q + 1))
+            copy = nc.scalar.copy if q == 0 else nc.vector.tensor_copy
+            copy(imp_win[:, cols].rearrange("p (n c) -> p n c", c=4), imp_ps[:].rearrange("p c n -> p n c"))
 
         weight = sb.tile([P, I], F32, name="weight")
         nc.vector.tensor_tensor(weight[:], imp_win[:].indirect(offsets[:]), pf_slots[:], MULT)
 
-        b_grp = sb.tile([P, G, PACK], BF16, name="b_grp", align_bytes=64)
-        back = ps.tile([P, PE_PLANES, G], F32, name="back", tag="bank7")
-        for t in range(PACK):
-            x = sb.tile([P, I], F32, name=f"x{t}")
-            nc.vector.tensor_tensor(x[:], key_planes[t][:].indirect(offsets[:]), weight[:], MULT)
-            x_pages = x[:].rearrange("p (g j) -> p g j", j=PAGE)
-            if t < PE_PLANES:
-                sums = ps.tile([P, P], F32, name=f"sums{t}", tag=f"bank{5 + t}")
-                for j in range(PAGE):
-                    nc.tensor.matmul(sums[:], x_pages[:, :, j], ident[:], start=(j == 0), stop=(j == PAGE - 1), is_transpose=True)
-                turned = sb.tile([P, P], F32, name=f"turned{t}")
-                nc.scalar.copy(turned[:], sums[:])
-                nc.tensor.transpose(back[:, t, :], turned[:], ident[:])
-                if t == PE_PLANES - 1:
-                    nc.scalar.copy(b_grp[:, :, 0:PE_PLANES], back[:].rearrange("p t g -> p g t"))
-            else:
-                with nc.allow_low_precision(reason="float32 sum, rounded once for the quantiser"):
-                    nc.vector.tensor_reduce(b_grp[:, :, t], x_pages, AXIS_X, ADD)
-
         w_codes = sb.tile([P, PACK, P], U32, name="w_codes", align_bytes=64)
         w_scales = sb.tile([P, PACK, P], U8, name="w_scales", align_bytes=64)
-        for h in range(2):
-            grp = sb.tile([P, PACK, 64, PACK], BF16, name=f"w_grp{h}", align_bytes=64)
-            nc.scalar.copy(grp[:].rearrange("p t s j -> p s j t"), wd_raw[h][:].rearrange("p j (s t) -> p s j t", t=PACK))
-            for t in range(PACK):
-                nc.vector.quantize_mx(out=w_codes[:, t, 64 * h:64 * h + 64].bitcast(FP8X4),
-                                      scales=w_scales[:, t, 64 * h:64 * h + 64],
-                                      in_=grp[:, t].rearrange("p s j -> p (s j)"))
+
+        w_grp = sb.tile([P, PACK, P, PACK], BF16, name="w_grp", tag="pf_slots", align_bytes=64)
+
+        def group_wd(h):
+            nc.scalar.copy(w_grp[:, :, 64 * h:64 * h + 64, :].rearrange("p t s j -> p s j t"),
+                           wd_raw[h][:].rearrange("p j (s t) -> p s j t", t=PACK))
+
+        def gather(t):
+            x = sb.tile([P, I], F32, name=f"x{t}")
+            nc.vector.tensor_tensor(x[:], key_planes[t][:].indirect(offsets[:]), weight[:], MULT)
+            return x[:].rearrange("p (g j) -> p g j", j=PAGE)
+
+        def sum_pages(t, x_pages):
+            sums = ps.tile([P, P], F32, name=f"sums{t}", tag=f"bank{3 + t}")
+            for j in range(PAGE):
+                nc.tensor.matmul(sums[:], x_pages[:, :, j], ident[:], start=(j == 0), stop=(j == PAGE - 1), is_transpose=True)
+            return sums
+
+        def turn_back(t, sums, tag, back):
+            turned = sb.tile([P, P], F32, name=f"turned{t}", tag=tag)
+            nc.scalar.copy(turned[:], sums[:])
+            nc.tensor.transpose(back, turned[:], ident[:])
+
+        b_sums = sb.tile([P, PACK, G], F32, name="b_sums")
+        back_a = ps.tile([P, G], F32, name="back_a", tag="bank6")
+        back_b = ps.tile([P, 2, G], F32, name="back_b", tag="bank7")
+        group_wd(0)
+        sums0 = sum_pages(0, gather(0))
+        sums1 = sum_pages(1, gather(1))
+        turn_back(0, sums0, "keys1", back_a[:])
+        nc.scalar.copy(b_sums[:, 0, :], back_a[:])
+        sums2 = sum_pages(2, gather(2))
+        turn_back(1, sums1, "keys2", back_b[:, 0, :])
+        nc.vector.tensor_reduce(b_sums[:, 3, :], gather(3), AXIS_X, ADD)
+        group_wd(1)
+        for t in range(PACK):
+            nc.vector.quantize_mx(out=w_codes[:, t, :].bitcast(FP8X4), scales=w_scales[:, t, :],
+                                  in_=w_grp[:, t].rearrange("p s j -> p (s j)"))
+        turn_back(2, sums2, "wd_raw1", back_b[:, 1, :])
+        nc.scalar.copy(b_sums[:, 1:3, :], back_b[:])
+        b_grp = sb.tile([P, G, PACK], BF16, name="b_grp", align_bytes=64)
+        nc.vector.tensor_copy(b_grp[:].rearrange("p (c i) t -> p c t i", i=4), b_sums[:].rearrange("p t (c i) -> p c t i", i=4))
 
         b_codes = sb.tile([P, G], U32, name="b_codes", align_bytes=64)
         b_scales = sb.tile([P, G], U8, name="b_scales", align_bytes=64)
@@ -106,16 +119,14 @@ def tile_attend_pagesummary_pl_kernel(tc, keys, imp, pf, wd, offs, out_0, out_1,
 
         y = sb.tile([P, PACK, G], F32, name="y")
         out_rows = out_0.rearrange("(p t) g -> p t g", t=PACK)
-        for u in range(2):
-            acc = ps.tile([P, 2, G], F32, name=f"acc{u}", tag=f"bank{u}")
-            for v in range(2):
-                t = 2 * u + v
-                nc.tensor.matmul_mx(out=acc[:, v, :], lhsT=w_codes[:, t, :].bitcast(FP8X4), lhsT_scale=w_scales[:, t, :],
-                                    rhs=b_codes[:].bitcast(FP8X4), rhs_scale=b_scales[:], start=True, stop=True)
-            if u == 0:
-                nc.scalar.copy(y[:, 0:2, :], acc[:])
+        for t in range(PACK):
+            acc = ps.tile([P, G], F32, name=f"acc{t}", tag=f"bank{t}")
+            nc.tensor.matmul_mx(out=acc[:], lhsT=w_codes[:, t, :].bitcast(FP8X4), lhsT_scale=w_scales[:, t, :],
+                                rhs=b_codes[:].bitcast(FP8X4), rhs_scale=b_scales[:], start=True, stop=True)
+            if t % 2 == 0:
+                nc.scalar.copy(y[:, t, :], acc[:])
             else:
-                nc.vector.tensor_copy(y[:, 2:4, :], acc[:])
+                nc.vector.tensor_copy(y[:, t, :], acc[:])
         nc.sync.dma_start(out_rows, y[:])
 
         y_grp = sb.tile([P, G, PACK], BF16, name="y_grp", align_bytes=64)

@@ -37,81 +37,67 @@ def tile_attend_pagesummary_pl_kernel(tc, keys, imp, pf, wd, offs, out_0, out_1,
         nc.sync.dma_start(imp_cols[:], imp[0, IMP_DMA:T].rearrange("(q p c) -> p q c", q=2, c=4))
         nc.sync.dma_start(imp_win[:, 0:IMP_DMA], imp[:, 0:IMP_DMA])
         nc.sync.dma_start(offsets[:], offs)
-        wd_raw = [sb.tile([P, PACK, M // 2], F32, name=f"wd_raw{h}", tag=f"wd_raw{h}") for h in range(2)]
-        wd_halves = [wd[:, h * 256:(h + 1) * 256].rearrange("(p j) m -> p j m", j=PACK) for h in range(2)]
-        nc.sync.dma_start(wd_raw[0][:], wd_halves[0])
         key_rows = keys.rearrange("(p t) n -> t p n", t=PACK)
-        key_planes = []
-        for t in range(PACK):
-            plane = sb.tile([P, T], F32, name=f"keys{t}", tag=f"keys{t}")
-            nc.sync.dma_start(plane[:], key_rows[t])
-            key_planes.append(plane)
-        nc.sync.dma_start(wd_raw[1][:], wd_halves[1])
+        key_planes = [sb.tile([P, T], F32, name=f"keys{t}") for t in range(PACK)]
+        wd_raw = sb.tile([P, PACK, M], F32, name="wd_raw")
+        for t in range(2):
+            nc.sync.dma_start(key_planes[t][:], key_rows[t])
+        nc.sync.dma_start(wd_raw[:], wd.rearrange("(p j) m -> p j m", j=PACK))
+        for t in range(2, PACK):
+            nc.sync.dma_start(key_planes[t][:], key_rows[t])
 
         ident = sb.tile([P, P], F32, name="ident")
         make_identity(nc, ident[:])
 
         pf_ps = ps.tile([P, G], F32, name="pf_ps", tag="bank2")
         nc.tensor.transpose(pf_ps[:], pf_col[:].to_broadcast([P, P]), ident[:])
-        pf_slots = sb.tile([P, I], F32, name="pf_slots", tag="pf_slots", align_bytes=64)
-        nc.vector.tensor_copy(pf_slots[:].rearrange("p (g j) -> p g j", j=PAGE),
-                              pf_ps[:].unsqueeze(2).to_broadcast([P, G, PAGE]))
+        pf_slots = sb.tile([P, I], F32, name="pf_slots")
+        nc.scalar.copy(pf_slots[:].rearrange("p (g j) -> p g j", j=PAGE),
+                       pf_ps[:].unsqueeze(2).to_broadcast([P, G, PAGE]))
 
         for q in range(2):
             imp_ps = ps.tile([P, 4, P], F32, name=f"imp_ps{q}", tag=f"bank{q}")
             for c in range(4):
                 nc.tensor.transpose(imp_ps[:, c, :], imp_cols[:, q, c:c + 1].to_broadcast([P, P]), ident[:])
             cols = slice(IMP_DMA + 512 * q, IMP_DMA + 512 * (q + 1))
-            copy = nc.scalar.copy if q == 0 else nc.vector.tensor_copy
-            copy(imp_win[:, cols].rearrange("p (n c) -> p n c", c=4), imp_ps[:].rearrange("p c n -> p n c"))
+            nc.vector.tensor_copy(imp_win[:, cols].rearrange("p (n c) -> p n c", c=4), imp_ps[:].rearrange("p c n -> p n c"))
 
         weight = sb.tile([P, I], F32, name="weight")
         nc.vector.tensor_tensor(weight[:], imp_win[:].indirect(offsets[:]), pf_slots[:], MULT)
 
         w_codes = sb.tile([P, PACK, P], U32, name="w_codes", align_bytes=64)
         w_scales = sb.tile([P, PACK, P], U8, name="w_scales", align_bytes=64)
-
-        w_grp = sb.tile([P, PACK, P, PACK], BF16, name="w_grp", tag="pf_slots", align_bytes=64)
-
-        def group_wd(h):
-            nc.scalar.copy(w_grp[:, :, 64 * h:64 * h + 64, :].rearrange("p t s j -> p s j t"),
-                           wd_raw[h][:].rearrange("p j (s t) -> p s j t", t=PACK))
+        w_grp = sb.tile([P, PACK, P, PACK], BF16, name="w_grp", align_bytes=64)
+        b_grp = sb.tile([P, G, PACK], BF16, name="b_grp", align_bytes=64)
 
         def gather(t):
             x = sb.tile([P, I], F32, name=f"x{t}")
             nc.vector.tensor_tensor(x[:], key_planes[t][:].indirect(offsets[:]), weight[:], MULT)
             return x[:].rearrange("p (g j) -> p g j", j=PAGE)
 
-        def sum_pages(t, x_pages):
-            sums = ps.tile([P, P], F32, name=f"sums{t}", tag=f"bank{3 + t}")
+        back = ps.tile([P, 2, G], F32, name="back", tag="bank6")
+        for t in range(2):
+            x_pages = gather(t)
+            sums = ps.tile([P, P], F32, name=f"sums{t}", tag=f"bank{4 + t}")
             for j in range(PAGE):
                 nc.tensor.matmul(sums[:], x_pages[:, :, j], ident[:], start=(j == 0), stop=(j == PAGE - 1), is_transpose=True)
-            return sums
-
-        def turn_back(t, sums, tag, back):
-            turned = sb.tile([P, P], F32, name=f"turned{t}", tag=tag)
+            turned = sb.tile([P, P], F32, name=f"turned{t}")
             nc.scalar.copy(turned[:], sums[:])
-            nc.tensor.transpose(back, turned[:], ident[:])
+            nc.tensor.transpose(back[:, t, :], turned[:], ident[:])
+        nc.scalar.copy(b_grp[:, :, 0:2], back[:].rearrange("p t g -> p g t"))
 
-        b_sums = sb.tile([P, PACK, G], F32, name="b_sums")
-        back_a = ps.tile([P, G], F32, name="back_a", tag="bank6")
-        back_b = ps.tile([P, 2, G], F32, name="back_b", tag="bank7")
-        group_wd(0)
-        sums0 = sum_pages(0, gather(0))
-        sums1 = sum_pages(1, gather(1))
-        turn_back(0, sums0, "keys1", back_a[:])
-        nc.scalar.copy(b_sums[:, 0, :], back_a[:])
-        sums2 = sum_pages(2, gather(2))
-        turn_back(1, sums1, "keys2", back_b[:, 0, :])
-        nc.vector.tensor_reduce(b_sums[:, 3, :], gather(3), AXIS_X, ADD)
-        group_wd(1)
-        for t in range(PACK):
-            nc.vector.quantize_mx(out=w_codes[:, t, :].bitcast(FP8X4), scales=w_scales[:, t, :],
-                                  in_=w_grp[:, t].rearrange("p s j -> p (s j)"))
-        turn_back(2, sums2, "wd_raw1", back_b[:, 1, :])
-        nc.scalar.copy(b_sums[:, 1:3, :], back_b[:])
-        b_grp = sb.tile([P, G, PACK], BF16, name="b_grp", align_bytes=64)
-        nc.vector.tensor_copy(b_grp[:].rearrange("p (c i) t -> p c t i", i=4), b_sums[:].rearrange("p t (c i) -> p c t i", i=4))
+        nc.scalar.copy(w_grp[:].rearrange("p t s j -> p s j t"), wd_raw[:].rearrange("p j (s t) -> p s j t", t=PACK))
+
+        def reduce_pages(t):
+            x_pages = gather(t)
+            with nc.allow_low_precision(reason="float32 sum, rounded once on the way to the quantiser"):
+                nc.vector.tensor_reduce(b_grp[:, :, t], x_pages, AXIS_X, ADD)
+
+        reduce_pages(2)
+        nc.vector.quantize_mx(out=w_codes[:].rearrange("p t s -> p (t s)").bitcast(FP8X4),
+                              scales=w_scales[:].rearrange("p t s -> p (t s)"),
+                              in_=w_grp[:].rearrange("p t s j -> p (t s j)"))
+        reduce_pages(3)
 
         b_codes = sb.tile([P, G], U32, name="b_codes", align_bytes=64)
         b_scales = sb.tile([P, G], U8, name="b_scales", align_bytes=64)

@@ -20,7 +20,7 @@ AXIS_X = mybir.AxisListType.X
 P = 128
 PACK = 4
 PAGE = I // G
-IMP_DMA = 1024
+IMP_DMA = 1536
 
 
 def tile_attend_pagesummary_pl_kernel(tc, keys, imp, pf, wd, offs, out_0, out_1, out_2):
@@ -30,54 +30,57 @@ def tile_attend_pagesummary_pl_kernel(tc, keys, imp, pf, wd, offs, out_0, out_1,
         ps = ctx.enter_context(tc.psum_pool(name="ps", bufs=1))
 
         offsets = sb.tile([P, I // 16], U16, name="offsets")
-        imp_cols = sb.tile([P, 2, 4], F32, name="imp_cols")
+        imp_cols = sb.tile([P, 4], F32, name="imp_cols")
         imp_win = sb.tile([P, T], F32, name="imp_win")
         pf_col = sb.tile([P, 1], F32, name="pf_col")
         nc.sync.dma_start(pf_col[:], pf.rearrange("o g -> g o"))
-        nc.sync.dma_start(imp_cols[:], imp[0, IMP_DMA:T].rearrange("(q p c) -> p q c", q=2, c=4))
+        nc.sync.dma_start(imp_cols[:], imp[0, IMP_DMA:T].rearrange("(p c) -> p c", c=4))
         nc.sync.dma_start(imp_win[:, 0:IMP_DMA], imp[:, 0:IMP_DMA])
         nc.sync.dma_start(offsets[:], offs)
         key_rows = keys.rearrange("(p t) n -> t p n", t=PACK)
         key_planes = [sb.tile([P, T], F32, name=f"keys{t}") for t in range(PACK)]
-        wd_raw = sb.tile([P, PACK, M], F32, name="wd_raw")
-        for t in range(2):
+        wd_raw = [sb.tile([P, PACK, M // 2], F32, name=f"wd_raw{h}") for h in range(2)]
+        wd_halves = [wd[:, h * 256:(h + 1) * 256].rearrange("(p j) m -> p j m", j=PACK) for h in range(2)]
+        for t in range(3):
             nc.sync.dma_start(key_planes[t][:], key_rows[t])
-        nc.sync.dma_start(wd_raw[:], wd.rearrange("(p j) m -> p j m", j=PACK))
-        for t in range(2, PACK):
-            nc.sync.dma_start(key_planes[t][:], key_rows[t])
+        nc.sync.dma_start(wd_raw[0][:], wd_halves[0])
+        nc.sync.dma_start(key_planes[3][:], key_rows[3])
+        nc.sync.dma_start(wd_raw[1][:], wd_halves[1])
 
         ident = sb.tile([P, P], F32, name="ident")
         make_identity(nc, ident[:])
 
         pf_ps = ps.tile([P, G], F32, name="pf_ps", tag="bank2")
         nc.tensor.transpose(pf_ps[:], pf_col[:].to_broadcast([P, P]), ident[:])
-        pf_slots = sb.tile([P, I], F32, name="pf_slots")
-        nc.scalar.copy(pf_slots[:].rearrange("p (g j) -> p g j", j=PAGE),
-                       pf_ps[:].unsqueeze(2).to_broadcast([P, G, PAGE]))
-
-        for q in range(2):
-            imp_ps = ps.tile([P, 4, P], F32, name=f"imp_ps{q}", tag=f"bank{q}")
-            for c in range(4):
-                nc.tensor.transpose(imp_ps[:, c, :], imp_cols[:, q, c:c + 1].to_broadcast([P, P]), ident[:])
-            cols = slice(IMP_DMA + 512 * q, IMP_DMA + 512 * (q + 1))
-            nc.vector.tensor_copy(imp_win[:, cols].rearrange("p (n c) -> p n c", c=4), imp_ps[:].rearrange("p c n -> p n c"))
+        imp_ps = ps.tile([P, 4, P], F32, name="imp_ps", tag="bank0")
+        for c in range(4):
+            nc.tensor.transpose(imp_ps[:, c, :], imp_cols[:, c:c + 1].to_broadcast([P, P]), ident[:])
+        nc.vector.tensor_copy(imp_win[:, IMP_DMA:T].rearrange("p (n c) -> p n c", c=4), imp_ps[:].rearrange("p c n -> p n c"))
 
         weight = sb.tile([P, I], F32, name="weight")
-        nc.vector.tensor_tensor(weight[:], imp_win[:].indirect(offsets[:]), pf_slots[:], MULT)
+        for h in range(2):
+            pf_slots = sb.tile([P, G // 2, PAGE], F32, name=f"pf_slots{h}")
+            nc.scalar.copy(pf_slots[:], pf_ps[:, 64 * h:64 * h + 64].unsqueeze(2).to_broadcast([P, G // 2, PAGE]))
+            nc.vector.tensor_tensor(weight[:, 512 * h:512 * h + 512], imp_win[:].indirect(offsets[:, 32 * h:32 * h + 32]),
+                                    pf_slots[:].rearrange("p g j -> p (g j)"), MULT)
 
         w_codes = sb.tile([P, PACK, P], U32, name="w_codes", align_bytes=64)
         w_scales = sb.tile([P, PACK, P], U8, name="w_scales", align_bytes=64)
         w_grp = sb.tile([P, PACK, P, PACK], BF16, name="w_grp", align_bytes=64)
         b_grp = sb.tile([P, G, PACK], BF16, name="b_grp", align_bytes=64)
 
-        def gather(t):
-            x = sb.tile([P, I], F32, name=f"x{t}")
-            nc.vector.tensor_tensor(x[:], key_planes[t][:].indirect(offsets[:]), weight[:], MULT)
-            return x[:].rearrange("p (g j) -> p g j", j=PAGE)
+        def gather(t, x, h, n):
+            slots = slice(h * I // n, (h + 1) * I // n)
+            cols = slice(h * I // n // 16, (h + 1) * I // n // 16)
+            nc.vector.tensor_tensor(x[:, slots], key_planes[t][:].indirect(offsets[:, cols]), weight[:, slots], MULT)
 
         back = ps.tile([P, 2, G], F32, name="back", tag="bank6")
         for t in range(2):
-            x_pages = gather(t)
+            x = sb.tile([P, I], F32, name=f"x{t}")
+            pieces = 2 - t
+            for h in range(pieces):
+                gather(t, x, h, pieces)
+            x_pages = x[:].rearrange("p (g j) -> p g j", j=PAGE)
             sums = ps.tile([P, P], F32, name=f"sums{t}", tag=f"bank{4 + t}")
             for j in range(PAGE):
                 nc.tensor.matmul(sums[:], x_pages[:, :, j], ident[:], start=(j == 0), stop=(j == PAGE - 1), is_transpose=True)
@@ -86,40 +89,54 @@ def tile_attend_pagesummary_pl_kernel(tc, keys, imp, pf, wd, offs, out_0, out_1,
             nc.tensor.transpose(back[:, t, :], turned[:], ident[:])
         nc.scalar.copy(b_grp[:, :, 0:2], back[:].rearrange("p t g -> p g t"))
 
-        nc.scalar.copy(w_grp[:].rearrange("p t s j -> p s j t"), wd_raw[:].rearrange("p j (s t) -> p s j t", t=PACK))
+        for h in range(2):
+            nc.scalar.copy(w_grp[:, :, 64 * h:64 * h + 64, :].rearrange("p t s j -> p s j t"),
+                           wd_raw[h][:].rearrange("p j (s t) -> p s j t", t=PACK))
 
-        def reduce_pages(t):
-            x_pages = gather(t)
-            with nc.allow_low_precision(reason="float32 sum, rounded once on the way to the quantiser"):
-                nc.vector.tensor_reduce(b_grp[:, :, t], x_pages, AXIS_X, ADD)
+        for t in range(2, PACK):
+            x = sb.tile([P, I], F32, name=f"x{t}")
+            x_pages = x[:].rearrange("p (g j) -> p g j", j=PAGE)
+            for h in range(2):
+                gather(t, x, h, 2)
+            for h in range(2):
+                pages = slice(64 * h, 64 * h + 64)
+                with nc.allow_low_precision(reason="float32 sum, rounded once on the way to the quantiser"):
+                    nc.vector.tensor_reduce(b_grp[:, pages, t], x_pages[:, pages, :], AXIS_X, ADD)
 
-        reduce_pages(2)
-        nc.vector.quantize_mx(out=w_codes[:].rearrange("p t s -> p (t s)").bitcast(FP8X4),
-                              scales=w_scales[:].rearrange("p t s -> p (t s)"),
-                              in_=w_grp[:].rearrange("p t s j -> p (t s j)"))
-        reduce_pages(3)
+        def quantise_wd(t):
+            nc.vector.quantize_mx(out=w_codes[:, t, :].bitcast(FP8X4), scales=w_scales[:, t, :],
+                                  in_=w_grp[:, t].rearrange("p s j -> p (s j)"))
 
         b_codes = sb.tile([P, G], U32, name="b_codes", align_bytes=64)
-        b_scales = sb.tile([P, G], U8, name="b_scales", align_bytes=64)
-        nc.vector.quantize_mx(out=b_codes[:].bitcast(FP8X4), scales=b_scales[:], in_=b_grp[:].rearrange("p g t -> p (g t)"))
+        b_scales = w_scales[4:P, 0, :]
+        quantise_wd(0)
+        quantise_wd(1)
+        nc.vector.quantize_mx(out=b_codes[:].bitcast(FP8X4), scales=b_scales, in_=b_grp[:].rearrange("p g t -> p (g t)"))
+        quantise_wd(2)
+        quantise_wd(3)
 
         y = sb.tile([P, PACK, G], F32, name="y")
         out_rows = out_0.rearrange("(p t) g -> p t g", t=PACK)
         for t in range(PACK):
             acc = ps.tile([P, G], F32, name=f"acc{t}", tag=f"bank{t}")
             nc.tensor.matmul_mx(out=acc[:], lhsT=w_codes[:, t, :].bitcast(FP8X4), lhsT_scale=w_scales[:, t, :],
-                                rhs=b_codes[:].bitcast(FP8X4), rhs_scale=b_scales[:], start=True, stop=True)
-            if t % 2 == 0:
+                                rhs=b_codes[:].bitcast(FP8X4), rhs_scale=b_scales, start=True, stop=True)
+            if t % 2 == 1:
                 nc.scalar.copy(y[:, t, :], acc[:])
             else:
                 nc.vector.tensor_copy(y[:, t, :], acc[:])
         nc.sync.dma_start(out_rows, y[:])
 
         y_grp = sb.tile([P, G, PACK], BF16, name="y_grp", align_bytes=64)
-        nc.vector.tensor_copy(y_grp[:].rearrange("p (c i) t -> p c t i", i=4), y[:].rearrange("p t (c i) -> p c t i", i=4))
         y_codes = sb.tile([P, G], U32, name="y_codes", align_bytes=64)
         y_scales = sb.tile([P, G], U8, name="y_scales", align_bytes=64)
-        nc.vector.quantize_mx(out=y_codes[:].bitcast(FP8X4), scales=y_scales[:], in_=y_grp[:].rearrange("p g t -> p (g t)"))
+        halves = [slice(0, G // 2), slice(G // 2, G)]
+        for pages in halves:
+            nc.vector.tensor_copy(y_grp[:, pages, :].rearrange("p (c i) t -> p c t i", i=4),
+                                  y[:, :, pages].rearrange("p t (c i) -> p c t i", i=4))
+        for pages in halves:
+            nc.vector.quantize_mx(out=y_codes[:, pages].bitcast(FP8X4), scales=y_scales[:, pages],
+                                  in_=y_grp[:, pages, :].rearrange("p g t -> p (g t)"))
         nc.sync.dma_start(out_1[0].rearrange("p c r -> p (c r)").bitcast(I32), y_codes[:].bitcast(I32))
         for q in range(4):
             queue = nc.sync if q < 2 else nc.scalar

@@ -20,7 +20,8 @@ AXIS_X = mybir.AxisListType.X
 P = 128
 PACK = 4
 PAGE = I // G
-IMP_DMA = 1536
+LAST = P - 1
+PIECES = [128, 128, 256, 256, 256]
 
 
 def tile_attend_pagesummary_pl_kernel(tc, keys, imp, pf, wd, offs, out_0, out_1, out_2):
@@ -30,78 +31,91 @@ def tile_attend_pagesummary_pl_kernel(tc, keys, imp, pf, wd, offs, out_0, out_1,
         ps = ctx.enter_context(tc.psum_pool(name="ps", bufs=1))
 
         offsets = sb.tile([P, I // 16], U16, name="offsets")
-        imp_cols = sb.tile([P, 4], F32, name="imp_cols")
         imp_win = sb.tile([P, T], F32, name="imp_win")
-        pf_col = sb.tile([P, 1], F32, name="pf_col")
-        nc.sync.dma_start(pf_col[:], pf.rearrange("o g -> g o"))
-        nc.sync.dma_start(imp_cols[:], imp[0, IMP_DMA:T].rearrange("(p c) -> p c", c=4))
-        nc.sync.dma_start(imp_win[:, 0:IMP_DMA], imp[:, 0:IMP_DMA])
+        pf_row = sb.tile([P, G], F32, name="pf_row")
         nc.sync.dma_start(offsets[:], offs)
+        nc.sync.dma_start(pf_row[LAST:P, :], pf)
+        nc.sync.dma_start(imp_win[LAST:P, :], imp[0:1, :])
         key_rows = keys.rearrange("(p t) n -> t p n", t=PACK)
         key_planes = [sb.tile([P, T], F32, name=f"keys{t}") for t in range(PACK)]
-        wd_raw = [sb.tile([P, PACK, M // 2], F32, name=f"wd_raw{h}") for h in range(2)]
-        wd_halves = [wd[:, h * 256:(h + 1) * 256].rearrange("(p j) m -> p j m", j=PACK) for h in range(2)]
-        for t in range(3):
+        for t in (2, 0, 1, 3):
             nc.sync.dma_start(key_planes[t][:], key_rows[t])
-        nc.sync.dma_start(wd_raw[0][:], wd_halves[0])
-        nc.sync.dma_start(key_planes[3][:], key_rows[3])
-        nc.sync.dma_start(wd_raw[1][:], wd_halves[1])
+        wd_rows = wd.rearrange("(p j) m -> p j m", j=PACK)
+        wd_raw = [sb.tile([P, 2, M], F32, name=f"wd_raw{h}", tag=f"wd_raw{h}") for h in range(2)]
+        for h in range(2):
+            nc.sync.dma_start(wd_raw[h][:], wd_rows[:, 2 * h:2 * h + 2, :])
 
+        nc.vector.memset(imp_win[0:LAST, 0:G], 0.0)
+        nc.vector.memset(imp_win[0:LAST, G:T], 0.0)
+        nc.scalar.copy(pf_row[0:LAST, :], imp_win[0:LAST, 0:G])
         ident = sb.tile([P, P], F32, name="ident")
         make_identity(nc, ident[:])
 
-        pf_ps = ps.tile([P, G], F32, name="pf_ps", tag="bank2")
-        nc.tensor.transpose(pf_ps[:], pf_col[:].to_broadcast([P, P]), ident[:])
-        imp_ps = ps.tile([P, 4, P], F32, name="imp_ps", tag="bank0")
-        for c in range(4):
-            nc.tensor.transpose(imp_ps[:, c, :], imp_cols[:, c:c + 1].to_broadcast([P, P]), ident[:])
-        nc.vector.tensor_copy(imp_win[:, IMP_DMA:T].rearrange("p (n c) -> p n c", c=4), imp_ps[:].rearrange("p c n -> p n c"))
+        def list_cols(first, count):
+            return offsets[:, first // 16:(first + count) // 16]
 
         weight = sb.tile([P, I], F32, name="weight")
-        for h in range(2):
-            pf_slots = sb.tile([P, G // 2, PAGE], F32, name=f"pf_slots{h}")
-            nc.scalar.copy(pf_slots[:], pf_ps[:, 64 * h:64 * h + 64].unsqueeze(2).to_broadcast([P, G // 2, PAGE]))
-            nc.vector.tensor_tensor(weight[:, 512 * h:512 * h + 512], imp_win[:].indirect(offsets[:, 32 * h:32 * h + 32]),
-                                    pf_slots[:].rearrange("p g j -> p (g j)"), MULT)
+        starts = [sum(PIECES[:q]) for q in range(len(PIECES))]
+        pf_slots = [sb.tile([P, n // PAGE, PAGE], F32, name=f"pf_slots{q}") for q, n in enumerate(PIECES)]
+        for q, (first, n) in enumerate(zip(starts, PIECES)):
+            pages = slice(first // PAGE, (first + n) // PAGE)
+            nc.scalar.copy(pf_slots[q][:], pf_row[:, pages].unsqueeze(2).to_broadcast([P, n // PAGE, PAGE]))
+        for q, (first, n) in enumerate(zip(starts, PIECES)):
+            w_row = sb.tile([P, n], F32, name=f"w_row{q}")
+            nc.vector.tensor_tensor(w_row[:], imp_win[:].indirect(list_cols(first, n)),
+                                    pf_slots[q][:].rearrange("p g j -> p (g j)"), MULT)
+            for c in range(n // P):
+                block = first // P + c
+                cols = ps.tile([P, P], F32, name=f"cols{block}", tag=f"bank{block % 4}")
+                nc.tensor.transpose(cols[:], w_row[:, c * P:(c + 1) * P], ident[:])
+                w_col = sb.tile([P, 1], F32, name=f"w_col{block}")
+                nc.scalar.copy(w_col[:], cols[:, LAST:P])
+                spread = ps.tile([P, P], F32, name=f"spread{block}", tag=f"bank{4 + block % 4}")
+                nc.tensor.transpose(spread[:], w_col[:].to_broadcast([P, P]), ident[:])
+                nc.scalar.copy(weight[:, block * P:(block + 1) * P], spread[:])
 
         w_codes = sb.tile([P, PACK, P], U32, name="w_codes", align_bytes=64)
         w_scales = sb.tile([P, PACK, P], U8, name="w_scales", align_bytes=64)
         w_grp = sb.tile([P, PACK, P, PACK], BF16, name="w_grp", align_bytes=64)
         b_grp = sb.tile([P, G, PACK], BF16, name="b_grp", align_bytes=64)
 
-        def gather(t, x, h, n):
-            slots = slice(h * I // n, (h + 1) * I // n)
-            cols = slice(h * I // n // 16, (h + 1) * I // n // 16)
-            nc.vector.tensor_tensor(x[:, slots], key_planes[t][:].indirect(offsets[:, cols]), weight[:, slots], MULT)
-
-        back = ps.tile([P, 2, G], F32, name="back", tag="bank6")
-        for t in range(2):
+        def gather(t, pieces):
             x = sb.tile([P, I], F32, name=f"x{t}")
-            pieces = 2 - t
-            for h in range(pieces):
-                gather(t, x, h, pieces)
-            x_pages = x[:].rearrange("p (g j) -> p g j", j=PAGE)
-            sums = ps.tile([P, P], F32, name=f"sums{t}", tag=f"bank{4 + t}")
+            for h, count in enumerate(pieces):
+                first = sum(pieces[:h])
+                nc.vector.tensor_tensor(x[:, first:first + count], key_planes[t][:].indirect(list_cols(first, count)),
+                                        weight[:, first:first + count], MULT)
+            return x[:].rearrange("p (g j) -> p g j", j=PAGE)
+
+        def sum_pages(t, x_pages, back, bank, tag):
+            sums = ps.tile([P, P], F32, name=f"sums{t}", tag=bank)
             for j in range(PAGE):
                 nc.tensor.matmul(sums[:], x_pages[:, :, j], ident[:], start=(j == 0), stop=(j == PAGE - 1), is_transpose=True)
-            turned = sb.tile([P, P], F32, name=f"turned{t}")
+            turned = sb.tile([P, P], F32, name=f"turned{t}", tag=tag)
             nc.scalar.copy(turned[:], sums[:])
-            nc.tensor.transpose(back[:, t, :], turned[:], ident[:])
-        nc.scalar.copy(b_grp[:, :, 0:2], back[:].rearrange("p t g -> p g t"))
+            nc.tensor.transpose(back, turned[:], ident[:])
 
+        def round_wd(h, s0, s1):
+            nc.scalar.copy(w_grp[:, :, s0:s1, 2 * h:2 * h + 2].rearrange("p t s j -> p s j t"),
+                           wd_raw[h][:, :, PACK * s0:PACK * s1].rearrange("p j (s t) -> p s j t", t=PACK))
+
+        back2 = ps.tile([P, G], F32, name="back2", tag="bank6")
+        sum_pages(2, gather(2, PIECES), back2[:], "bank0", "turned2")
+        nc.scalar.copy(b_grp[:, :, 2:4], back2[:].unsqueeze(2).to_broadcast([P, G, 2]))
+        back01 = ps.tile([P, 2, G], F32, name="back01", tag="bank7")
+        sum_pages(0, gather(0, [I]), back01[:, 0, :], "bank1", "turned0")
+        x1 = gather(1, [I])
+        round_wd(0, 0, P)
+        sum_pages(1, x1, back01[:, 1, :], "bank0", "wd_raw0")
+        round_wd(1, 0, P // 2)
+        round_wd(1, P // 2, P)
+        nc.scalar.copy(b_grp[:, :, 0:2], back01[:].rearrange("p t g -> p g t"))
+
+        x3 = gather(3, [I // 2, I // 2])
         for h in range(2):
-            nc.scalar.copy(w_grp[:, :, 64 * h:64 * h + 64, :].rearrange("p t s j -> p s j t"),
-                           wd_raw[h][:].rearrange("p j (s t) -> p s j t", t=PACK))
-
-        for t in range(2, PACK):
-            x = sb.tile([P, I], F32, name=f"x{t}")
-            x_pages = x[:].rearrange("p (g j) -> p g j", j=PAGE)
-            for h in range(2):
-                gather(t, x, h, 2)
-            for h in range(2):
-                pages = slice(64 * h, 64 * h + 64)
-                with nc.allow_low_precision(reason="float32 sum, rounded once on the way to the quantiser"):
-                    nc.vector.tensor_reduce(b_grp[:, pages, t], x_pages[:, pages, :], AXIS_X, ADD)
+            pages = slice(64 * h, 64 * h + 64)
+            with nc.allow_low_precision(reason="float32 sum, rounded once on the way to the quantiser"):
+                nc.vector.tensor_reduce(b_grp[:, pages, 3], x3[:, pages, :], AXIS_X, ADD)
 
         def quantise_wd(t):
             nc.vector.quantize_mx(out=w_codes[:, t, :].bitcast(FP8X4), scales=w_scales[:, t, :],

@@ -38,12 +38,12 @@ def tile_attend_pagesummary_pl_kernel(tc, keys, imp, pf, wd, offs, out_0, out_1,
         nc.sync.dma_start(imp_win[LAST:P, :], imp[0:1, :])
         key_rows = keys.rearrange("(p t) n -> t p n", t=PACK)
         key_planes = [sb.tile([P, T], F32, name=f"keys{t}") for t in range(PACK)]
-        for t in (2, 0, 1, 3):
+        wd_raw = sb.tile([P, PACK, M], F32, name="wd_raw")
+        for t in (2, 0):
             nc.sync.dma_start(key_planes[t][:], key_rows[t])
-        wd_rows = wd.rearrange("(p j) m -> p j m", j=PACK)
-        wd_raw = [sb.tile([P, 2, M], F32, name=f"wd_raw{h}", tag=f"wd_raw{h}") for h in range(2)]
-        for h in range(2):
-            nc.sync.dma_start(wd_raw[h][:], wd_rows[:, 2 * h:2 * h + 2, :])
+        nc.sync.dma_start(wd_raw[:], wd.rearrange("(p j) m -> p j m", j=PACK))
+        for t in (1, 3):
+            nc.sync.dma_start(key_planes[t][:], key_rows[t])
 
         nc.vector.memset(imp_win[0:LAST, 0:G], 0.0)
         nc.vector.memset(imp_win[0:LAST, G:T], 0.0)
@@ -54,7 +54,7 @@ def tile_attend_pagesummary_pl_kernel(tc, keys, imp, pf, wd, offs, out_0, out_1,
         def list_cols(first, count):
             return offsets[:, first // 16:(first + count) // 16]
 
-        weight = sb.tile([P, I], F32, name="weight")
+        weight = sb.tile([P, I], F32, name="weight", tag="weight", align_bytes=64)
         starts = [sum(PIECES[:q]) for q in range(len(PIECES))]
         pf_slots = [sb.tile([P, n // PAGE, PAGE], F32, name=f"pf_slots{q}") for q, n in enumerate(PIECES)]
         for q, (first, n) in enumerate(zip(starts, PIECES)):
@@ -74,7 +74,6 @@ def tile_attend_pagesummary_pl_kernel(tc, keys, imp, pf, wd, offs, out_0, out_1,
                 nc.tensor.transpose(spread[:], w_col[:].to_broadcast([P, P]), ident[:])
                 nc.scalar.copy(weight[:, block * P:(block + 1) * P], spread[:])
 
-        w_codes = sb.tile([P, PACK, P], U32, name="w_codes", align_bytes=64)
         w_scales = sb.tile([P, PACK, P], U8, name="w_scales", align_bytes=64)
         w_grp = sb.tile([P, PACK, P, PACK], BF16, name="w_grp", align_bytes=64)
         b_grp = sb.tile([P, G, PACK], BF16, name="b_grp", align_bytes=64)
@@ -95,20 +94,19 @@ def tile_attend_pagesummary_pl_kernel(tc, keys, imp, pf, wd, offs, out_0, out_1,
             nc.scalar.copy(turned[:], sums[:])
             nc.tensor.transpose(back, turned[:], ident[:])
 
-        def round_wd(h, s0, s1):
-            nc.scalar.copy(w_grp[:, :, s0:s1, 2 * h:2 * h + 2].rearrange("p t s j -> p s j t"),
-                           wd_raw[h][:, :, PACK * s0:PACK * s1].rearrange("p j (s t) -> p s j t", t=PACK))
+        def round_wd(q):
+            s0, s1 = q * P // 4, (q + 1) * P // 4
+            nc.scalar.copy(w_grp[:, :, s0:s1, :].rearrange("p t s j -> p s j t"),
+                           wd_raw[:, :, PACK * s0:PACK * s1].rearrange("p j (s t) -> p s j t", t=PACK))
 
         back2 = ps.tile([P, G], F32, name="back2", tag="bank6")
         sum_pages(2, gather(2, PIECES), back2[:], "bank0", "turned2")
         nc.scalar.copy(b_grp[:, :, 2:4], back2[:].unsqueeze(2).to_broadcast([P, G, 2]))
         back01 = ps.tile([P, 2, G], F32, name="back01", tag="bank7")
         sum_pages(0, gather(0, [I]), back01[:, 0, :], "bank1", "turned0")
-        x1 = gather(1, [I])
-        round_wd(0, 0, P)
-        sum_pages(1, x1, back01[:, 1, :], "bank0", "wd_raw0")
-        round_wd(1, 0, P // 2)
-        round_wd(1, P // 2, P)
+        for q in range(4):
+            round_wd(q)
+        sum_pages(1, gather(1, [I]), back01[:, 1, :], "bank0", "turned1")
         nc.scalar.copy(b_grp[:, :, 0:2], back01[:].rearrange("p t g -> p g t"))
 
         x3 = gather(3, [I // 2, I // 2])
@@ -116,6 +114,8 @@ def tile_attend_pagesummary_pl_kernel(tc, keys, imp, pf, wd, offs, out_0, out_1,
             pages = slice(64 * h, 64 * h + 64)
             with nc.allow_low_precision(reason="float32 sum, rounded once on the way to the quantiser"):
                 nc.vector.tensor_reduce(b_grp[:, pages, 3], x3[:, pages, :], AXIS_X, ADD)
+
+        w_codes = sb.tile([P, PACK, P], U32, name="w_codes", tag="weight", align_bytes=64)
 
         def quantise_wd(t):
             nc.vector.quantize_mx(out=w_codes[:, t, :].bitcast(FP8X4), scales=w_scales[:, t, :],

@@ -37,12 +37,11 @@ def tile_attend_pagesummary_pl_kernel(tc, keys, imp, pf, wd, offs, out_0, out_1,
         nc.sync.dma_start(pf_row[LAST:P, :], pf)
         nc.sync.dma_start(imp_win[LAST:P, :], imp[0:1, :])
         key_rows = keys.rearrange("(p t) n -> t p n", t=PACK)
-        key_planes = [sb.tile([P, T], F32, name=f"keys{t}") for t in range(PACK)]
+        key_planes = [sb.tile([P, T], F32, name=f"keys{t}", tag=f"keys{t}") for t in range(PACK)]
         wd_raw = sb.tile([P, PACK, M], F32, name="wd_raw")
-        for t in (2, 0):
-            nc.sync.dma_start(key_planes[t][:], key_rows[t])
+        nc.sync.dma_start(key_planes[2][:], key_rows[2])
         nc.sync.dma_start(wd_raw[:], wd.rearrange("(p j) m -> p j m", j=PACK))
-        for t in (1, 3):
+        for t in (0, 1, 3):
             nc.sync.dma_start(key_planes[t][:], key_rows[t])
 
         nc.vector.memset(imp_win[0:LAST, 0:G], 0.0)
@@ -68,18 +67,18 @@ def tile_attend_pagesummary_pl_kernel(tc, keys, imp, pf, wd, offs, out_0, out_1,
                 block = first // P + c
                 cols = ps.tile([P, P], F32, name=f"cols{block}", tag=f"bank{block % 4}")
                 nc.tensor.transpose(cols[:], w_row[:, c * P:(c + 1) * P], ident[:])
-                w_col = sb.tile([P, 1], F32, name=f"w_col{block}")
+                w_col = sb.tile([P, 1], F32, name=f"w_col{block}", tag=f"w_col{block}", align_bytes=64)
                 nc.scalar.copy(w_col[:], cols[:, LAST:P])
                 spread = ps.tile([P, P], F32, name=f"spread{block}", tag=f"bank{4 + block % 4}")
                 nc.tensor.transpose(spread[:], w_col[:].to_broadcast([P, P]), ident[:])
                 nc.scalar.copy(weight[:, block * P:(block + 1) * P], spread[:])
 
         w_scales = sb.tile([P, PACK, P], U8, name="w_scales", align_bytes=64)
-        w_grp = sb.tile([P, PACK, P, PACK], BF16, name="w_grp", align_bytes=64)
+        w_grp = [sb.tile([P, 2, P, PACK], BF16, name="w_grp01", tag="w_col7", align_bytes=64)]
         b_grp = sb.tile([P, G, PACK], BF16, name="b_grp", align_bytes=64)
 
         def gather(t, pieces):
-            x = sb.tile([P, I], F32, name=f"x{t}")
+            x = sb.tile([P, I], F32, name=f"x{t}", tag=f"x{t}", align_bytes=64)
             for h, count in enumerate(pieces):
                 first = sum(pieces[:h])
                 nc.vector.tensor_tensor(x[:, first:first + count], key_planes[t][:].indirect(list_cols(first, count)),
@@ -94,20 +93,25 @@ def tile_attend_pagesummary_pl_kernel(tc, keys, imp, pf, wd, offs, out_0, out_1,
             nc.scalar.copy(turned[:], sums[:])
             nc.tensor.transpose(back, turned[:], ident[:])
 
-        def round_wd(q):
-            s0, s1 = q * P // 4, (q + 1) * P // 4
-            nc.scalar.copy(w_grp[:, :, s0:s1, :].rearrange("p t s j -> p s j t"),
-                           wd_raw[:, :, PACK * s0:PACK * s1].rearrange("p j (s t) -> p s j t", t=PACK))
+        def round_wd(t):
+            nc.scalar.copy(w_grp[t // 2][:, t % 2], wd_raw[:].rearrange("p j (s t) -> p t s j", t=PACK)[:, t])
 
+        round_wd(0)
+        round_wd(1)
         back2 = ps.tile([P, G], F32, name="back2", tag="bank6")
         sum_pages(2, gather(2, PIECES), back2[:], "bank0", "turned2")
+        w_grp.append(sb.tile([P, 2, P, PACK], BF16, name="w_grp23", tag="x2", align_bytes=64))
+        round_wd(2)
         nc.scalar.copy(b_grp[:, :, 2:4], back2[:].unsqueeze(2).to_broadcast([P, G, 2]))
-        back01 = ps.tile([P, 2, G], F32, name="back01", tag="bank7")
-        sum_pages(0, gather(0, [I]), back01[:, 0, :], "bank1", "turned0")
-        for q in range(4):
-            round_wd(q)
-        sum_pages(1, gather(1, [I]), back01[:, 1, :], "bank0", "turned1")
-        nc.scalar.copy(b_grp[:, :, 0:2], back01[:].rearrange("p t g -> p g t"))
+        round_wd(3)
+        x0 = gather(0, [I])
+        x1 = gather(1, [I])
+        back0 = ps.tile([P, G], F32, name="back0", tag="bank7")
+        sum_pages(0, x0, back0[:], "bank1", "keys1")
+        nc.scalar.copy(b_grp[:, :, 0], back0[:])
+        back1 = ps.tile([P, G], F32, name="back1", tag="bank6")
+        sum_pages(1, x1, back1[:], "bank0", "turned1")
+        nc.scalar.copy(b_grp[:, :, 1], back1[:])
 
         x3 = gather(3, [I // 2, I // 2])
         for h in range(2):
@@ -119,7 +123,7 @@ def tile_attend_pagesummary_pl_kernel(tc, keys, imp, pf, wd, offs, out_0, out_1,
 
         def quantise_wd(t):
             nc.vector.quantize_mx(out=w_codes[:, t, :].bitcast(FP8X4), scales=w_scales[:, t, :],
-                                  in_=w_grp[:, t].rearrange("p s j -> p (s j)"))
+                                  in_=w_grp[t // 2][:, t % 2].rearrange("p s j -> p (s j)"))
 
         b_codes = sb.tile([P, G], U32, name="b_codes", align_bytes=64)
         b_scales = w_scales[4:P, 0, :]

@@ -37,12 +37,11 @@ def tile_attend_pagesummary_pl_kernel(tc, keys, imp, pf, wd, offs, out_0, out_1,
         nc.sync.dma_start(pf_row[LAST:P, :], pf)
         nc.sync.dma_start(imp_win[LAST:P, :], imp[0:1, :])
         key_rows = keys.rearrange("(p t) n -> t p n", t=PACK)
-        key_planes = [sb.tile([P, T], F32, name=f"keys{t}", tag=f"keys{t}") for t in range(PACK)]
+        key_planes = [sb.tile([P, T], F32, name=f"keys{t}") for t in range(PACK)]
         wd_raw = sb.tile([P, PACK, M], F32, name="wd_raw")
-        nc.sync.dma_start(key_planes[2][:], key_rows[2])
-        nc.sync.dma_start(wd_raw[:], wd.rearrange("(p j) m -> p j m", j=PACK))
-        for t in (0, 1, 3):
+        for t in (2, 0, 1, 3):
             nc.sync.dma_start(key_planes[t][:], key_rows[t])
+        nc.sync.dma_start(wd_raw[:], wd.rearrange("(p j) m -> p j m", j=PACK))
 
         nc.vector.memset(imp_win[0:LAST, 0:G], 0.0)
         nc.vector.memset(imp_win[0:LAST, G:T], 0.0)
@@ -53,7 +52,7 @@ def tile_attend_pagesummary_pl_kernel(tc, keys, imp, pf, wd, offs, out_0, out_1,
         def list_cols(first, count):
             return offsets[:, first // 16:(first + count) // 16]
 
-        weight = sb.tile([P, I], F32, name="weight", tag="weight", align_bytes=64)
+        weight = sb.tile([P, I], F32, name="weight")
         starts = [sum(PIECES[:q]) for q in range(len(PIECES))]
         pf_slots = [sb.tile([P, n // PAGE, PAGE], F32, name=f"pf_slots{q}") for q, n in enumerate(PIECES)]
         for q, (first, n) in enumerate(zip(starts, PIECES)):
@@ -67,51 +66,46 @@ def tile_attend_pagesummary_pl_kernel(tc, keys, imp, pf, wd, offs, out_0, out_1,
                 block = first // P + c
                 cols = ps.tile([P, P], F32, name=f"cols{block}", tag=f"bank{block % 4}")
                 nc.tensor.transpose(cols[:], w_row[:, c * P:(c + 1) * P], ident[:])
-                w_col = sb.tile([P, 1], F32, name=f"w_col{block}", tag=f"w_col{block}", align_bytes=64)
+                w_col = sb.tile([P, 1], F32, name=f"w_col{block}")
                 nc.scalar.copy(w_col[:], cols[:, LAST:P])
                 spread = ps.tile([P, P], F32, name=f"spread{block}", tag=f"bank{4 + block % 4}")
                 nc.tensor.transpose(spread[:], w_col[:].to_broadcast([P, P]), ident[:])
                 nc.scalar.copy(weight[:, block * P:(block + 1) * P], spread[:])
 
         w_scales = sb.tile([P, PACK, P], U8, name="w_scales", align_bytes=64)
-        w_grp = [sb.tile([P, 2, P, PACK], BF16, name="w_grp01", tag="w_col7", align_bytes=64)]
+        w_grp = sb.tile([P, PACK, P, PACK], BF16, name="w_grp", align_bytes=64)
         b_grp = sb.tile([P, G, PACK], BF16, name="b_grp", align_bytes=64)
 
         def gather(t, pieces):
-            x = sb.tile([P, I], F32, name=f"x{t}", tag=f"x{t}", align_bytes=64)
+            x = sb.tile([P, I], F32, name=f"x{t}")
             for h, count in enumerate(pieces):
                 first = sum(pieces[:h])
                 nc.vector.tensor_tensor(x[:, first:first + count], key_planes[t][:].indirect(list_cols(first, count)),
                                         weight[:, first:first + count], MULT)
             return x[:].rearrange("p (g j) -> p g j", j=PAGE)
 
-        def sum_pages(t, x_pages, back, bank, tag):
-            sums = ps.tile([P, P], F32, name=f"sums{t}", tag=bank)
+        def sum_pages(sums, x_pages):
             for j in range(PAGE):
-                nc.tensor.matmul(sums[:], x_pages[:, :, j], ident[:], start=(j == 0), stop=(j == PAGE - 1), is_transpose=True)
-            turned = sb.tile([P, P], F32, name=f"turned{t}", tag=tag)
-            nc.scalar.copy(turned[:], sums[:])
-            nc.tensor.transpose(back, turned[:], ident[:])
+                nc.tensor.matmul(sums, x_pages[:, :, j], ident[:], start=(j == 0), stop=(j == PAGE - 1), is_transpose=True)
 
-        def round_wd(t):
-            nc.scalar.copy(w_grp[t // 2][:, t % 2], wd_raw[:].rearrange("p j (s t) -> p t s j", t=PACK)[:, t])
+        def turn_back(pairs, bank):
+            back = ps.tile([P, G], F32, name=f"back_{bank}", tag=bank)
+            nc.tensor.transpose(back[:], pairs[:].rearrange("g p e -> g (p e)").bitcast(F32), ident[:])
+            return back
 
-        round_wd(0)
-        round_wd(1)
-        back2 = ps.tile([P, G], F32, name="back2", tag="bank6")
-        sum_pages(2, gather(2, PIECES), back2[:], "bank0", "turned2")
-        w_grp.append(sb.tile([P, 2, P, PACK], BF16, name="w_grp23", tag="x2", align_bytes=64))
-        round_wd(2)
-        nc.scalar.copy(b_grp[:, :, 2:4], back2[:].unsqueeze(2).to_broadcast([P, G, 2]))
-        round_wd(3)
-        x0 = gather(0, [I])
-        x1 = gather(1, [I])
-        back0 = ps.tile([P, G], F32, name="back0", tag="bank7")
-        sum_pages(0, x0, back0[:], "bank1", "keys1")
-        nc.scalar.copy(b_grp[:, :, 0], back0[:])
-        back1 = ps.tile([P, G], F32, name="back1", tag="bank6")
-        sum_pages(1, x1, back1[:], "bank0", "turned1")
-        nc.scalar.copy(b_grp[:, :, 1], back1[:])
+        b_words = b_grp[:].rearrange("p g t -> p (g t)").bitcast(F32).rearrange("p (g u) -> p g u", u=2)
+
+        sums = ps.tile([P, P], F32, name="sums2", tag="bank0")
+        sum_pages(sums[:], gather(2, PIECES))
+        pairs = sb.tile([P, P, 2], BF16, name="pairs23")
+        nc.scalar.copy(pairs[:], sums[:].unsqueeze(2).to_broadcast([P, P, 2]))
+        nc.scalar.copy(b_words, turn_back(pairs, "bank6")[:].unsqueeze(2).to_broadcast([P, G, 2]))
+        sums = ps.tile([P, 2, P], F32, name="sums01", tag="bank1")
+        for t in range(2):
+            sum_pages(sums[:, t, :], gather(t, [I]))
+        pairs = sb.tile([P, P, 2], BF16, name="pairs01")
+        nc.scalar.copy(pairs[:], sums[:].rearrange("g e p -> g p e"))
+        nc.scalar.copy(b_words[:, :, 0], turn_back(pairs, "bank7")[:])
 
         x3 = gather(3, [I // 2, I // 2])
         for h in range(2):
@@ -119,26 +113,26 @@ def tile_attend_pagesummary_pl_kernel(tc, keys, imp, pf, wd, offs, out_0, out_1,
             with nc.allow_low_precision(reason="float32 sum, rounded once on the way to the quantiser"):
                 nc.vector.tensor_reduce(b_grp[:, pages, 3], x3[:, pages, :], AXIS_X, ADD)
 
-        w_codes = sb.tile([P, PACK, P], U32, name="w_codes", tag="weight", align_bytes=64)
+        for q in range(4):
+            s0, s1 = q * P // 4, (q + 1) * P // 4
+            copy = nc.scalar.copy if q < 2 else nc.vector.tensor_copy
+            copy(w_grp[:, :, s0:s1, :].rearrange("p t s j -> p s j t"),
+                 wd_raw[:, :, PACK * s0:PACK * s1].rearrange("p j (s t) -> p s j t", t=PACK))
 
-        def quantise_wd(t):
-            nc.vector.quantize_mx(out=w_codes[:, t, :].bitcast(FP8X4), scales=w_scales[:, t, :],
-                                  in_=w_grp[t // 2][:, t % 2].rearrange("p s j -> p (s j)"))
-
+        w_codes = sb.tile([P, PACK, P], U32, name="w_codes", align_bytes=64)
         b_codes = sb.tile([P, G], U32, name="b_codes", align_bytes=64)
-        b_scales = w_scales[4:P, 0, :]
-        quantise_wd(0)
-        quantise_wd(1)
-        nc.vector.quantize_mx(out=b_codes[:].bitcast(FP8X4), scales=b_scales, in_=b_grp[:].rearrange("p g t -> p (g t)"))
-        quantise_wd(2)
-        quantise_wd(3)
+        b_scales = sb.tile([P, G], U8, name="b_scales", align_bytes=64)
+        nc.vector.quantize_mx(out=b_codes[:].bitcast(FP8X4), scales=b_scales[:], in_=b_grp[:].rearrange("p g t -> p (g t)"))
+        for t in range(PACK):
+            nc.vector.quantize_mx(out=w_codes[:, t, :].bitcast(FP8X4), scales=w_scales[:, t, :],
+                                  in_=w_grp[:, t].rearrange("p s j -> p (s j)"))
 
         y = sb.tile([P, PACK, G], F32, name="y")
         out_rows = out_0.rearrange("(p t) g -> p t g", t=PACK)
         for t in range(PACK):
             acc = ps.tile([P, G], F32, name=f"acc{t}", tag=f"bank{t}")
             nc.tensor.matmul_mx(out=acc[:], lhsT=w_codes[:, t, :].bitcast(FP8X4), lhsT_scale=w_scales[:, t, :],
-                                rhs=b_codes[:].bitcast(FP8X4), rhs_scale=b_scales, start=True, stop=True)
+                                rhs=b_codes[:].bitcast(FP8X4), rhs_scale=b_scales[:], start=True, stop=True)
             if t % 2 == 1:
                 nc.scalar.copy(y[:, t, :], acc[:])
             else:

@@ -22,6 +22,7 @@ PACK = 4
 PAGE = I // G
 LAST = P - 1
 PIECES = [128, 128, 256, 256, 256]
+SPLIT = 72
 
 
 def tile_attend_pagesummary_pl_kernel(tc, keys, imp, pf, wd, offs, out_0, out_1, out_2):
@@ -39,7 +40,7 @@ def tile_attend_pagesummary_pl_kernel(tc, keys, imp, pf, wd, offs, out_0, out_1,
         key_rows = keys.rearrange("(p t) n -> t p n", t=PACK)
         key_planes = [sb.tile([P, T], F32, name=f"keys{t}") for t in range(PACK)]
         wd_raw = sb.tile([P, PACK, M], F32, name="wd_raw")
-        for t in (2, 0, 1, 3):
+        for t in range(PACK):
             nc.sync.dma_start(key_planes[t][:], key_rows[t])
         nc.sync.dma_start(wd_raw[:], wd.rearrange("(p j) m -> p j m", j=PACK))
 
@@ -95,27 +96,21 @@ def tile_attend_pagesummary_pl_kernel(tc, keys, imp, pf, wd, offs, out_0, out_1,
 
         b_words = b_grp[:].rearrange("p g t -> p (g t)").bitcast(F32).rearrange("p (g u) -> p g u", u=2)
 
-        sums = ps.tile([P, P], F32, name="sums2", tag="bank0")
-        sum_pages(sums[:], gather(2, PIECES))
-        pairs = sb.tile([P, P, 2], BF16, name="pairs23")
-        nc.scalar.copy(pairs[:], sums[:].unsqueeze(2).to_broadcast([P, P, 2]))
-        nc.scalar.copy(b_words, turn_back(pairs, "bank6")[:].unsqueeze(2).to_broadcast([P, G, 2]))
-        sums = ps.tile([P, 2, P], F32, name="sums01", tag="bank1")
-        for t in range(2):
-            sum_pages(sums[:, t, :], gather(t, [I]))
-        pairs = sb.tile([P, P, 2], BF16, name="pairs01")
+        sums = ps.tile([P, 2, P], F32, name="sums", tag="bank0")
+        sum_pages(sums[:, 0, :], gather(0, PIECES))
+        sum_pages(sums[:, 1, :], gather(1, [I]))
+        pairs = sb.tile([P, P, 2], BF16, name="pairs")
         nc.scalar.copy(pairs[:], sums[:].rearrange("g e p -> g p e"))
         nc.scalar.copy(b_words[:, :, 0], turn_back(pairs, "bank7")[:])
 
-        x3 = gather(3, [I // 2, I // 2])
-        for h in range(2):
-            pages = slice(64 * h, 64 * h + 64)
-            with nc.allow_low_precision(reason="float32 sum, rounded once on the way to the quantiser"):
-                nc.vector.tensor_reduce(b_grp[:, pages, 3], x3[:, pages, :], AXIS_X, ADD)
+        for t in range(2, PACK):
+            x_pages = gather(t, [I // 2, I // 2])
+            for h in range(2):
+                pages = slice(64 * h, 64 * h + 64)
+                with nc.allow_low_precision(reason="float32 sum, rounded once on the way to the quantiser"):
+                    nc.vector.tensor_reduce(b_grp[:, pages, t], x_pages[:, pages, :], AXIS_X, ADD)
 
-        for q in range(4):
-            s0, s1 = q * P // 4, (q + 1) * P // 4
-            copy = nc.scalar.copy if q < 2 else nc.vector.tensor_copy
+        for copy, s0, s1 in ((nc.scalar.copy, 0, SPLIT), (nc.vector.tensor_copy, SPLIT, P)):
             copy(w_grp[:, :, s0:s1, :].rearrange("p t s j -> p s j t"),
                  wd_raw[:, :, PACK * s0:PACK * s1].rearrange("p j (s t) -> p s j t", t=PACK))
 

@@ -22,7 +22,7 @@ PACK = 4
 PAGE = I // G
 LAST = P - 1
 PIECES = [128, 128, 256, 256, 256]
-SPLIT = 72
+SPLIT = 56
 
 
 def tile_attend_pagesummary_pl_kernel(tc, keys, imp, pf, wd, offs, out_0, out_1, out_2):
@@ -39,7 +39,7 @@ def tile_attend_pagesummary_pl_kernel(tc, keys, imp, pf, wd, offs, out_0, out_1,
         nc.sync.dma_start(imp_win[LAST:P, :], imp[0:1, :])
         key_rows = keys.rearrange("(p t) n -> t p n", t=PACK)
         key_planes = [sb.tile([P, T], F32, name=f"keys{t}") for t in range(PACK)]
-        wd_raw = sb.tile([P, PACK, M], F32, name="wd_raw")
+        wd_raw = sb.tile([P, PACK, M], F32, name="wd_raw", tag="wd_raw", align_bytes=64)
         for t in range(PACK):
             nc.sync.dma_start(key_planes[t][:], key_rows[t])
         nc.sync.dma_start(wd_raw[:], wd.rearrange("(p j) m -> p j m", j=PACK))
@@ -115,7 +115,7 @@ def tile_attend_pagesummary_pl_kernel(tc, keys, imp, pf, wd, offs, out_0, out_1,
                  wd_raw[:, :, PACK * s0:PACK * s1].rearrange("p j (s t) -> p s j t", t=PACK))
 
         w_codes = sb.tile([P, PACK, P], U32, name="w_codes", align_bytes=64)
-        b_codes = sb.tile([P, G], U32, name="b_codes", align_bytes=64)
+        b_codes = sb.tile([P, G], U32, name="b_codes", tag="wd_raw", align_bytes=64)
         b_scales = sb.tile([P, G], U8, name="b_scales", align_bytes=64)
         nc.vector.quantize_mx(out=b_codes[:].bitcast(FP8X4), scales=b_scales[:], in_=b_grp[:].rearrange("p g t -> p (g t)"))
         for t in range(PACK):

@@ -22,7 +22,7 @@ PACK = 4
 PAGE = I // G
 LAST = P - 1
 PIECES = [128, 128, 256, 256, 256]
-SPLIT = 56
+SCALAR_PLACES = (62, 78)
 
 
 def tile_attend_pagesummary_pl_kernel(tc, keys, imp, pf, wd, offs, out_0, out_1, out_2):
@@ -39,7 +39,7 @@ def tile_attend_pagesummary_pl_kernel(tc, keys, imp, pf, wd, offs, out_0, out_1,
         nc.sync.dma_start(imp_win[LAST:P, :], imp[0:1, :])
         key_rows = keys.rearrange("(p t) n -> t p n", t=PACK)
         key_planes = [sb.tile([P, T], F32, name=f"keys{t}") for t in range(PACK)]
-        wd_raw = sb.tile([P, PACK, M], F32, name="wd_raw", tag="wd_raw", align_bytes=64)
+        wd_raw = sb.tile([P, PACK, M], F32, name="wd_raw")
         for t in range(PACK):
             nc.sync.dma_start(key_planes[t][:], key_rows[t])
         nc.sync.dma_start(wd_raw[:], wd.rearrange("(p j) m -> p j m", j=PACK))
@@ -73,9 +73,10 @@ def tile_attend_pagesummary_pl_kernel(tc, keys, imp, pf, wd, offs, out_0, out_1,
                 nc.tensor.transpose(spread[:], w_col[:].to_broadcast([P, P]), ident[:])
                 nc.scalar.copy(weight[:, block * P:(block + 1) * P], spread[:])
 
-        w_scales = sb.tile([P, PACK, P], U8, name="w_scales", align_bytes=64)
-        w_grp = sb.tile([P, PACK, P, PACK], BF16, name="w_grp", align_bytes=64)
-        b_grp = sb.tile([P, G, PACK], BF16, name="b_grp", align_bytes=64)
+        first_grp = sb.tile([P, 3, P, PACK], BF16, name="first_grp", align_bytes=64)
+        last_grp = sb.tile([P, 2, P, PACK], BF16, name="last_grp", align_bytes=64)
+        b_grp = first_grp[:, 0]
+        w_pairs = (first_grp[:, 1:3], last_grp[:])
 
         def gather(t, pieces):
             x = sb.tile([P, I], F32, name=f"x{t}")
@@ -94,7 +95,7 @@ def tile_attend_pagesummary_pl_kernel(tc, keys, imp, pf, wd, offs, out_0, out_1,
             nc.tensor.transpose(back[:], pairs[:].rearrange("g p e -> g (p e)").bitcast(F32), ident[:])
             return back
 
-        b_words = b_grp[:].rearrange("p g t -> p (g t)").bitcast(F32).rearrange("p (g u) -> p g u", u=2)
+        b_words = b_grp.rearrange("p g t -> p (g t)").bitcast(F32).rearrange("p (g u) -> p g u", u=2)
 
         sums = ps.tile([P, 2, P], F32, name="sums", tag="bank0")
         sum_pages(sums[:, 0, :], gather(0, PIECES))
@@ -110,25 +111,28 @@ def tile_attend_pagesummary_pl_kernel(tc, keys, imp, pf, wd, offs, out_0, out_1,
                 with nc.allow_low_precision(reason="float32 sum, rounded once on the way to the quantiser"):
                     nc.vector.tensor_reduce(b_grp[:, pages, t], x_pages[:, pages, :], AXIS_X, ADD)
 
-        for copy, s0, s1 in ((nc.scalar.copy, 0, SPLIT), (nc.vector.tensor_copy, SPLIT, P)):
-            copy(w_grp[:, :, s0:s1, :].rearrange("p t s j -> p s j t"),
-                 wd_raw[:, :, PACK * s0:PACK * s1].rearrange("p j (s t) -> p s j t", t=PACK))
+        wd_dealt = wd_raw[:].rearrange("p j (s u e) -> p u s j e", u=2, e=2)
+        for u, split in enumerate(SCALAR_PLACES):
+            nc.vector.tensor_copy(w_pairs[u][:, :, split:P, :].rearrange("p e s j -> p s j e"), wd_dealt[:, u, split:P])
+        for u, split in enumerate(SCALAR_PLACES):
+            nc.scalar.copy(w_pairs[u][:, :, 0:split, :].rearrange("p e s j -> p s j e"), wd_dealt[:, u, 0:split])
 
-        w_codes = sb.tile([P, PACK, P], U32, name="w_codes", align_bytes=64)
-        b_codes = sb.tile([P, G], U32, name="b_codes", tag="wd_raw", align_bytes=64)
-        b_scales = sb.tile([P, G], U8, name="b_scales", align_bytes=64)
-        nc.vector.quantize_mx(out=b_codes[:].bitcast(FP8X4), scales=b_scales[:], in_=b_grp[:].rearrange("p g t -> p (g t)"))
-        for t in range(PACK):
-            nc.vector.quantize_mx(out=w_codes[:, t, :].bitcast(FP8X4), scales=w_scales[:, t, :],
-                                  in_=w_grp[:, t].rearrange("p s j -> p (s j)"))
+        codes = sb.tile([P, 1 + PACK, P], U32, name="codes", align_bytes=64)
+        scales = sb.tile([P, 1 + PACK, P], U8, name="scales", align_bytes=64)
+        nc.vector.quantize_mx(out=codes[:, 0:2].rearrange("p a s -> p (a s)").bitcast(FP8X4),
+                              scales=scales[:, 0:2].rearrange("p a s -> p (a s)"),
+                              in_=first_grp[:, 0:2].rearrange("p a s j -> p (a s j)"))
+        for t in range(1, PACK):
+            nc.vector.quantize_mx(out=codes[:, 1 + t].bitcast(FP8X4), scales=scales[:, 1 + t],
+                                  in_=w_pairs[t // 2][:, t % 2].rearrange("p s j -> p (s j)"))
 
         y = sb.tile([P, PACK, G], F32, name="y")
         out_rows = out_0.rearrange("(p t) g -> p t g", t=PACK)
         for t in range(PACK):
             acc = ps.tile([P, G], F32, name=f"acc{t}", tag=f"bank{t}")
-            nc.tensor.matmul_mx(out=acc[:], lhsT=w_codes[:, t, :].bitcast(FP8X4), lhsT_scale=w_scales[:, t, :],
-                                rhs=b_codes[:].bitcast(FP8X4), rhs_scale=b_scales[:], start=True, stop=True)
-            if t % 2 == 1:
+            nc.tensor.matmul_mx(out=acc[:], lhsT=codes[:, 1 + t].bitcast(FP8X4), lhsT_scale=scales[:, 1 + t],
+                                rhs=codes[:, 0].bitcast(FP8X4), rhs_scale=scales[:, 0], start=True, stop=True)
+            if t != 2:
                 nc.scalar.copy(y[:, t, :], acc[:])
             else:
                 nc.vector.tensor_copy(y[:, t, :], acc[:])

@@ -126,25 +126,23 @@ def tile_attend_pagesummary_pl_kernel(tc, keys, imp, pf, wd, offs, out_0, out_1,
             nc.vector.quantize_mx(out=codes[:, 1 + t].bitcast(FP8X4), scales=scales[:, 1 + t],
                                   in_=w_pairs[t // 2][:, t % 2].rearrange("p s j -> p (s j)"))
 
+        halves = [slice(0, G // 2), slice(G // 2, G)]
         y = sb.tile([P, PACK, G], F32, name="y")
         out_rows = out_0.rearrange("(p t) g -> p t g", t=PACK)
         for t in range(PACK):
             acc = ps.tile([P, G], F32, name=f"acc{t}", tag=f"bank{t}")
             nc.tensor.matmul_mx(out=acc[:], lhsT=codes[:, 1 + t].bitcast(FP8X4), lhsT_scale=scales[:, 1 + t],
                                 rhs=codes[:, 0].bitcast(FP8X4), rhs_scale=scales[:, 0], start=True, stop=True)
-            if t != 2:
-                nc.scalar.copy(y[:, t, :], acc[:])
-            else:
-                nc.vector.tensor_copy(y[:, t, :], acc[:])
+            for pages in (halves if t == PACK - 1 else [slice(0, G)]):
+                nc.scalar.copy(y[:, t, pages], acc[:, pages])
         nc.sync.dma_start(out_rows, y[:])
 
         y_grp = sb.tile([P, G, PACK], BF16, name="y_grp", align_bytes=64)
         y_codes = sb.tile([P, G], U32, name="y_codes", align_bytes=64)
         y_scales = sb.tile([P, G], U8, name="y_scales", align_bytes=64)
-        halves = [slice(0, G // 2), slice(G // 2, G)]
-        for pages in halves:
-            nc.vector.tensor_copy(y_grp[:, pages, :].rearrange("p (c i) t -> p c t i", i=4),
-                                  y[:, :, pages].rearrange("p t (c i) -> p c t i", i=4))
+        for pages, rows in ((slice(0, G), slice(0, 2)), (halves[0], slice(2, 4)), (halves[1], slice(2, 4))):
+            nc.vector.tensor_copy(y_grp[:, pages, rows].rearrange("p (c i) t -> p c t i", i=4),
+                                  y[:, rows, pages].rearrange("p t (c i) -> p c t i", i=4))
         for pages in halves:
             nc.vector.quantize_mx(out=y_codes[:, pages].bitcast(FP8X4), scales=y_scales[:, pages],
                                   in_=y_grp[:, pages, :].rearrange("p g t -> p (g t)"))

@@ -16,13 +16,15 @@ FP8X4 = mybir.dt.float8_e4m3fn_x4
 MULT = mybir.AluOpType.mult
 ADD = mybir.AluOpType.add
 AXIS_X = mybir.AxisListType.X
+COPY = mybir.ActivationFunctionType.Copy
 
 P = 128
 PACK = 4
 PAGE = I // G
 LAST = P - 1
 PIECES = [128, 128, 256, 256, 256]
-SCALAR_PLACES = (62, 78)
+SCALAR_PLACES = (54, 72)
+VECTOR_SLOTS = [320, 512]
 
 
 def tile_attend_pagesummary_pl_kernel(tc, keys, imp, pf, wd, offs, out_0, out_1, out_2):
@@ -38,7 +40,7 @@ def tile_attend_pagesummary_pl_kernel(tc, keys, imp, pf, wd, offs, out_0, out_1,
         nc.sync.dma_start(pf_row[LAST:P, :], pf)
         nc.sync.dma_start(imp_win[LAST:P, :], imp[0:1, :])
         key_rows = keys.rearrange("(p t) n -> t p n", t=PACK)
-        key_planes = [sb.tile([P, T], F32, name=f"keys{t}") for t in range(PACK)]
+        key_planes = [sb.tile([P, T], F32, name=f"keys{t}", tag=f"keys{t}") for t in range(PACK)]
         wd_raw = sb.tile([P, PACK, M], F32, name="wd_raw")
         for t in range(PACK):
             nc.sync.dma_start(key_planes[t][:], key_rows[t])
@@ -79,7 +81,7 @@ def tile_attend_pagesummary_pl_kernel(tc, keys, imp, pf, wd, offs, out_0, out_1,
         w_pairs = (first_grp[:, 1:3], last_grp[:])
 
         def gather(t, pieces):
-            x = sb.tile([P, I], F32, name=f"x{t}")
+            x = sb.tile([P, sum(pieces)], F32, name=f"x{t}")
             for h, count in enumerate(pieces):
                 first = sum(pieces[:h])
                 nc.vector.tensor_tensor(x[:, first:first + count], key_planes[t][:].indirect(list_cols(first, count)),
@@ -100,16 +102,23 @@ def tile_attend_pagesummary_pl_kernel(tc, keys, imp, pf, wd, offs, out_0, out_1,
         sums = ps.tile([P, 2, P], F32, name="sums", tag="bank0")
         sum_pages(sums[:, 0, :], gather(0, PIECES))
         sum_pages(sums[:, 1, :], gather(1, [I]))
-        pairs = sb.tile([P, P, 2], BF16, name="pairs")
-        nc.scalar.copy(pairs[:], sums[:].rearrange("g e p -> g p e"))
-        nc.scalar.copy(b_words[:, :, 0], turn_back(pairs, "bank7")[:])
-
         for t in range(2, PACK):
-            x_pages = gather(t, [I // 2, I // 2])
-            for h in range(2):
-                pages = slice(64 * h, 64 * h + 64)
+            x_pages = gather(t, VECTOR_SLOTS)
+            first = sum(VECTOR_SLOTS)
+            raw = sb.tile([P, I - first], F32, name=f"raw{t}")
+            nc.scalar.activation(raw[:], key_planes[t][:].indirect(list_cols(first, I - first)), COPY)
+            x_rest = sb.tile([P, I - first], F32, name=f"x_rest{t}")
+            nc.gpsimd.tensor_tensor(x_rest[:], raw[:], weight[:, first:I], MULT)
+            cuts = [0, VECTOR_SLOTS[0] // PAGE, first // PAGE]
+            parts = [(slice(cuts[0], cuts[1]), x_pages[:, cuts[0]:cuts[1], :]), (slice(cuts[1], cuts[2]), x_pages[:, cuts[1]:cuts[2], :]),
+                     (slice(cuts[2], G), x_rest[:].rearrange("p (g j) -> p g j", j=PAGE))]
+            if t == 2:
+                pairs = sb.tile([P, P, 2], BF16, name="pairs", tag="keys2")
+                nc.scalar.copy(pairs[:], sums[:].rearrange("g e p -> g p e"))
+                nc.scalar.copy(b_words[:, :, 0], turn_back(pairs, "bank7")[:])
+            for pages, x_part in parts:
                 with nc.allow_low_precision(reason="float32 sum, rounded once on the way to the quantiser"):
-                    nc.vector.tensor_reduce(b_grp[:, pages, t], x_pages[:, pages, :], AXIS_X, ADD)
+                    nc.vector.tensor_reduce(b_grp[:, pages, t], x_part, AXIS_X, ADD)
 
         wd_dealt = wd_raw[:].rearrange("p j (s u e) -> p u s j e", u=2, e=2)
         for u, split in enumerate(SCALAR_PLACES):

@@ -23,7 +23,7 @@ PACK = 4
 PAGE = I // G
 LAST = P - 1
 PIECES = [128, 128, 256, 256, 256]
-SCALAR_PLACES = (54, 72)
+SCALAR_PLACES = (58, 76)
 VECTOR_SLOTS = [320, 512]
 
 
@@ -102,23 +102,26 @@ def tile_attend_pagesummary_pl_kernel(tc, keys, imp, pf, wd, offs, out_0, out_1,
         sums = ps.tile([P, 2, P], F32, name="sums", tag="bank0")
         sum_pages(sums[:, 0, :], gather(0, PIECES))
         sum_pages(sums[:, 1, :], gather(1, [I]))
-        for t in range(2, PACK):
-            x_pages = gather(t, VECTOR_SLOTS)
-            first = sum(VECTOR_SLOTS)
-            raw = sb.tile([P, I - first], F32, name=f"raw{t}")
-            nc.scalar.activation(raw[:], key_planes[t][:].indirect(list_cols(first, I - first)), COPY)
-            x_rest = sb.tile([P, I - first], F32, name=f"x_rest{t}")
-            nc.gpsimd.tensor_tensor(x_rest[:], raw[:], weight[:, first:I], MULT)
-            cuts = [0, VECTOR_SLOTS[0] // PAGE, first // PAGE]
-            parts = [(slice(cuts[0], cuts[1]), x_pages[:, cuts[0]:cuts[1], :]), (slice(cuts[1], cuts[2]), x_pages[:, cuts[1]:cuts[2], :]),
-                     (slice(cuts[2], G), x_rest[:].rearrange("p (g j) -> p g j", j=PAGE))]
-            if t == 2:
-                pairs = sb.tile([P, P, 2], BF16, name="pairs", tag="keys2")
-                nc.scalar.copy(pairs[:], sums[:].rearrange("g e p -> g p e"))
-                nc.scalar.copy(b_words[:, :, 0], turn_back(pairs, "bank7")[:])
-            for pages, x_part in parts:
-                with nc.allow_low_precision(reason="float32 sum, rounded once on the way to the quantiser"):
-                    nc.vector.tensor_reduce(b_grp[:, pages, t], x_part, AXIS_X, ADD)
+        def reduce_pages(t, first, x_pages):
+            with nc.allow_low_precision(reason="float32 sum, rounded once on the way to the quantiser"):
+                nc.vector.tensor_reduce(b_grp[:, first:first + x_pages.shape[1], t], x_pages, AXIS_X, ADD)
+
+        x_pages = gather(2, VECTOR_SLOTS)
+        rest = sum(VECTOR_SLOTS)
+        raw = sb.tile([P, I - rest], F32, name="raw")
+        nc.scalar.activation(raw[:], key_planes[2][:].indirect(list_cols(rest, I - rest)), COPY)
+        x_rest = sb.tile([P, I - rest], F32, name="x_rest")
+        nc.gpsimd.tensor_tensor(x_rest[:], raw[:], weight[:, rest:I], MULT)
+        pairs = sb.tile([P, P, 2], BF16, name="pairs", tag="keys2")
+        nc.scalar.copy(pairs[:], sums[:].rearrange("g e p -> g p e"))
+        nc.scalar.copy(b_words[:, :, 0], turn_back(pairs, "bank7")[:])
+        cut = VECTOR_SLOTS[0] // PAGE
+        reduce_pages(2, 0, x_pages[:, 0:cut, :])
+        reduce_pages(2, cut, x_pages[:, cut:rest // PAGE, :])
+        reduce_pages(2, rest // PAGE, x_rest[:].rearrange("p (g j) -> p g j", j=PAGE))
+        x_pages = gather(3, [I // 2, I // 2])
+        for first in (0, G // 2):
+            reduce_pages(3, first, x_pages[:, first:first + G // 2, :])
 
         wd_dealt = wd_raw[:].rearrange("p j (s u e) -> p u s j e", u=2, e=2)
         for u, split in enumerate(SCALAR_PLACES):

@@ -22,9 +22,10 @@ P = 128
 PACK = 4
 PAGE = I // G
 LAST = P - 1
-PIECES = [128, 128, 256, 256, 256]
-SCALAR_PLACES = (58, 76)
-VECTOR_SLOTS = [320, 512]
+GROUP = 16
+WEIGHT_PIECES = [128, 128, 256, 256, 256]
+VECTOR_SLOTS = {2: [320, 512], 3: [320, 608]}
+SCALAR_COLUMNS = (54, 72)
 
 
 def tile_attend_pagesummary_pl_kernel(tc, keys, imp, pf, wd, offs, out_0, out_1, out_2):
@@ -33,7 +34,7 @@ def tile_attend_pagesummary_pl_kernel(tc, keys, imp, pf, wd, offs, out_0, out_1,
         sb = ctx.enter_context(tc.tile_pool(name="sb", bufs=1))
         ps = ctx.enter_context(tc.psum_pool(name="ps", bufs=1))
 
-        offsets = sb.tile([P, I // 16], U16, name="offsets")
+        offsets = sb.tile([P, I // GROUP], U16, name="offsets")
         imp_win = sb.tile([P, T], F32, name="imp_win")
         pf_row = sb.tile([P, G], F32, name="pf_row")
         nc.sync.dma_start(offsets[:], offs)
@@ -53,32 +54,32 @@ def tile_attend_pagesummary_pl_kernel(tc, keys, imp, pf, wd, offs, out_0, out_1,
         make_identity(nc, ident[:])
 
         def list_cols(first, count):
-            return offsets[:, first // 16:(first + count) // 16]
+            return offsets[:, first // GROUP:(first + count) // GROUP]
 
         weight = sb.tile([P, I], F32, name="weight")
-        starts = [sum(PIECES[:q]) for q in range(len(PIECES))]
-        pf_slots = [sb.tile([P, n // PAGE, PAGE], F32, name=f"pf_slots{q}") for q, n in enumerate(PIECES)]
-        for q, (first, n) in enumerate(zip(starts, PIECES)):
+        starts = [sum(WEIGHT_PIECES[:q]) for q in range(len(WEIGHT_PIECES))]
+        pf_slots = [sb.tile([P, n // PAGE, PAGE], F32, name=f"pf_slots{q}") for q, n in enumerate(WEIGHT_PIECES)]
+        for q, (first, n) in enumerate(zip(starts, WEIGHT_PIECES)):
             pages = slice(first // PAGE, (first + n) // PAGE)
             nc.scalar.copy(pf_slots[q][:], pf_row[:, pages].unsqueeze(2).to_broadcast([P, n // PAGE, PAGE]))
-        for q, (first, n) in enumerate(zip(starts, PIECES)):
-            w_row = sb.tile([P, n], F32, name=f"w_row{q}")
-            nc.vector.tensor_tensor(w_row[:], imp_win[:].indirect(list_cols(first, n)),
+        for q, (first, n) in enumerate(zip(starts, WEIGHT_PIECES)):
+            weight_row = sb.tile([P, n], F32, name=f"weight_row{q}")
+            nc.vector.tensor_tensor(weight_row[:], imp_win[:].indirect(list_cols(first, n)),
                                     pf_slots[q][:].rearrange("p g j -> p (g j)"), MULT)
             for c in range(n // P):
                 block = first // P + c
                 cols = ps.tile([P, P], F32, name=f"cols{block}", tag=f"bank{block % 4}")
-                nc.tensor.transpose(cols[:], w_row[:, c * P:(c + 1) * P], ident[:])
-                w_col = sb.tile([P, 1], F32, name=f"w_col{block}")
-                nc.scalar.copy(w_col[:], cols[:, LAST:P])
+                nc.tensor.transpose(cols[:], weight_row[:, c * P:(c + 1) * P], ident[:])
+                weight_col = sb.tile([P, 1], F32, name=f"weight_col{block}")
+                nc.scalar.copy(weight_col[:], cols[:, LAST:P])
                 spread = ps.tile([P, P], F32, name=f"spread{block}", tag=f"bank{4 + block % 4}")
-                nc.tensor.transpose(spread[:], w_col[:].to_broadcast([P, P]), ident[:])
+                nc.tensor.transpose(spread[:], weight_col[:].to_broadcast([P, P]), ident[:])
                 nc.scalar.copy(weight[:, block * P:(block + 1) * P], spread[:])
 
         first_grp = sb.tile([P, 3, P, PACK], BF16, name="first_grp", align_bytes=64)
         last_grp = sb.tile([P, 2, P, PACK], BF16, name="last_grp", align_bytes=64)
         b_grp = first_grp[:, 0]
-        w_pairs = (first_grp[:, 1:3], last_grp[:])
+        wd_pairs = (first_grp[:, 1:3], last_grp[:])
 
         def gather(t, pieces):
             x = sb.tile([P, sum(pieces)], F32, name=f"x{t}")
@@ -88,46 +89,47 @@ def tile_attend_pagesummary_pl_kernel(tc, keys, imp, pf, wd, offs, out_0, out_1,
                                         weight[:, first:first + count], MULT)
             return x[:].rearrange("p (g j) -> p g j", j=PAGE)
 
-        def sum_pages(sums, x_pages):
-            for j in range(PAGE):
-                nc.tensor.matmul(sums, x_pages[:, :, j], ident[:], start=(j == 0), stop=(j == PAGE - 1), is_transpose=True)
+        def gather_rest(t, first):
+            raw = sb.tile([P, I - first], F32, name=f"raw{t}")
+            nc.scalar.activation(raw[:], key_planes[t][:].indirect(list_cols(first, I - first)), COPY)
+            x_rest = sb.tile([P, I - first], F32, name=f"x_rest{t}")
+            nc.gpsimd.tensor_tensor(x_rest[:], raw[:], weight[:, first:I], MULT)
+            return x_rest[:].rearrange("p (g j) -> p g j", j=PAGE)
 
-        def turn_back(pairs, bank):
-            back = ps.tile([P, G], F32, name=f"back_{bank}", tag=bank)
-            nc.tensor.transpose(back[:], pairs[:].rearrange("g p e -> g (p e)").bitcast(F32), ident[:])
-            return back
-
-        b_words = b_grp.rearrange("p g t -> p (g t)").bitcast(F32).rearrange("p (g u) -> p g u", u=2)
+        def reduce_pages(t, first_page, x_pages):
+            with nc.allow_low_precision(reason="float32 sum, rounded once on the way to the quantiser"):
+                nc.vector.tensor_reduce(b_grp[:, first_page:first_page + x_pages.shape[1], t], x_pages, AXIS_X, ADD)
 
         sums = ps.tile([P, 2, P], F32, name="sums", tag="bank0")
-        sum_pages(sums[:, 0, :], gather(0, PIECES))
-        sum_pages(sums[:, 1, :], gather(1, [I]))
-        def reduce_pages(t, first, x_pages):
-            with nc.allow_low_precision(reason="float32 sum, rounded once on the way to the quantiser"):
-                nc.vector.tensor_reduce(b_grp[:, first:first + x_pages.shape[1], t], x_pages, AXIS_X, ADD)
+        for t, pieces in enumerate((WEIGHT_PIECES, [I])):
+            x_pages = gather(t, pieces)
+            for j in range(PAGE):
+                nc.tensor.matmul(sums[:, t, :], x_pages[:, :, j], ident[:], start=(j == 0), stop=(j == PAGE - 1),
+                                 is_transpose=True)
 
-        x_pages = gather(2, VECTOR_SLOTS)
-        rest = sum(VECTOR_SLOTS)
-        raw = sb.tile([P, I - rest], F32, name="raw")
-        nc.scalar.activation(raw[:], key_planes[2][:].indirect(list_cols(rest, I - rest)), COPY)
-        x_rest = sb.tile([P, I - rest], F32, name="x_rest")
-        nc.gpsimd.tensor_tensor(x_rest[:], raw[:], weight[:, rest:I], MULT)
-        pairs = sb.tile([P, P, 2], BF16, name="pairs", tag="keys2")
-        nc.scalar.copy(pairs[:], sums[:].rearrange("g e p -> g p e"))
-        nc.scalar.copy(b_words[:, :, 0], turn_back(pairs, "bank7")[:])
-        cut = VECTOR_SLOTS[0] // PAGE
-        reduce_pages(2, 0, x_pages[:, 0:cut, :])
-        reduce_pages(2, cut, x_pages[:, cut:rest // PAGE, :])
-        reduce_pages(2, rest // PAGE, x_rest[:].rearrange("p (g j) -> p g j", j=PAGE))
-        x_pages = gather(3, [I // 2, I // 2])
-        for first in (0, G // 2):
-            reduce_pages(3, first, x_pages[:, first:first + G // 2, :])
+        def place_turned_sums():
+            pairs = sb.tile([P, P, 2], BF16, name="pairs", tag="keys2")
+            nc.scalar.copy(pairs[:], sums[:].rearrange("g e p -> g p e"))
+            back = ps.tile([P, G], F32, name="back", tag="bank7")
+            nc.tensor.transpose(back[:], pairs[:].rearrange("g p e -> g (p e)").bitcast(F32), ident[:])
+            b_words = b_grp.rearrange("p g t -> p (g t)").bitcast(F32).rearrange("p (g u) -> p g u", u=2)
+            nc.scalar.copy(b_words[:, :, 0], back[:])
+
+        for t, pieces in VECTOR_SLOTS.items():
+            x_pages = gather(t, pieces)
+            rest_pages = gather_rest(t, sum(pieces))
+            if t == 2:
+                place_turned_sums()
+            cut = pieces[0] // PAGE
+            reduce_pages(t, 0, x_pages[:, 0:cut, :])
+            reduce_pages(t, cut, x_pages[:, cut:sum(pieces) // PAGE, :])
+            reduce_pages(t, sum(pieces) // PAGE, rest_pages)
 
         wd_dealt = wd_raw[:].rearrange("p j (s u e) -> p u s j e", u=2, e=2)
-        for u, split in enumerate(SCALAR_PLACES):
-            nc.vector.tensor_copy(w_pairs[u][:, :, split:P, :].rearrange("p e s j -> p s j e"), wd_dealt[:, u, split:P])
-        for u, split in enumerate(SCALAR_PLACES):
-            nc.scalar.copy(w_pairs[u][:, :, 0:split, :].rearrange("p e s j -> p s j e"), wd_dealt[:, u, 0:split])
+        for u, split in enumerate(SCALAR_COLUMNS):
+            nc.vector.tensor_copy(wd_pairs[u][:, :, split:P, :].rearrange("p e s j -> p s j e"), wd_dealt[:, u, split:P])
+        for u, split in enumerate(SCALAR_COLUMNS):
+            nc.scalar.copy(wd_pairs[u][:, :, 0:split, :].rearrange("p e s j -> p s j e"), wd_dealt[:, u, 0:split])
 
         codes = sb.tile([P, 1 + PACK, P], U32, name="codes", align_bytes=64)
         scales = sb.tile([P, 1 + PACK, P], U8, name="scales", align_bytes=64)
@@ -136,25 +138,24 @@ def tile_attend_pagesummary_pl_kernel(tc, keys, imp, pf, wd, offs, out_0, out_1,
                               in_=first_grp[:, 0:2].rearrange("p a s j -> p (a s j)"))
         for t in range(1, PACK):
             nc.vector.quantize_mx(out=codes[:, 1 + t].bitcast(FP8X4), scales=scales[:, 1 + t],
-                                  in_=w_pairs[t // 2][:, t % 2].rearrange("p s j -> p (s j)"))
+                                  in_=wd_pairs[t // 2][:, t % 2].rearrange("p s j -> p (s j)"))
 
         halves = [slice(0, G // 2), slice(G // 2, G)]
         y = sb.tile([P, PACK, G], F32, name="y")
-        out_rows = out_0.rearrange("(p t) g -> p t g", t=PACK)
         for t in range(PACK):
             acc = ps.tile([P, G], F32, name=f"acc{t}", tag=f"bank{t}")
             nc.tensor.matmul_mx(out=acc[:], lhsT=codes[:, 1 + t].bitcast(FP8X4), lhsT_scale=scales[:, 1 + t],
                                 rhs=codes[:, 0].bitcast(FP8X4), rhs_scale=scales[:, 0], start=True, stop=True)
             for pages in (halves if t == PACK - 1 else [slice(0, G)]):
                 nc.scalar.copy(y[:, t, pages], acc[:, pages])
-        nc.sync.dma_start(out_rows, y[:])
+        nc.sync.dma_start(out_0.rearrange("(p t) g -> p t g", t=PACK), y[:])
 
         y_grp = sb.tile([P, G, PACK], BF16, name="y_grp", align_bytes=64)
         y_codes = sb.tile([P, G], U32, name="y_codes", align_bytes=64)
         y_scales = sb.tile([P, G], U8, name="y_scales", align_bytes=64)
-        for pages, rows in ((slice(0, G), slice(0, 2)), (halves[0], slice(2, 4)), (halves[1], slice(2, 4))):
-            nc.vector.tensor_copy(y_grp[:, pages, rows].rearrange("p (c i) t -> p c t i", i=4),
-                                  y[:, rows, pages].rearrange("p t (c i) -> p c t i", i=4))
+        for pages, places in ((slice(0, G), slice(0, 2)), (halves[0], slice(2, 4)), (halves[1], slice(2, 4))):
+            nc.vector.tensor_copy(y_grp[:, pages, places].rearrange("p (c i) t -> p c t i", i=4),
+                                  y[:, places, pages].rearrange("p t (c i) -> p c t i", i=4))
         for pages in halves:
             nc.vector.quantize_mx(out=y_codes[:, pages].bitcast(FP8X4), scales=y_scales[:, pages],
                                   in_=y_grp[:, pages, :].rearrange("p g t -> p (g t)"))

@@ -37,9 +37,9 @@ def tile_attend_pagesummary_pl_kernel(tc, keys, imp, pf, wd, offs, out_0, out_1,
         offsets = sb.tile([P, I // GROUP], U16, name="offsets")
         imp_win = sb.tile([P, T], F32, name="imp_win")
         pf_row = sb.tile([P, G], F32, name="pf_row")
-        nc.sync.dma_start(offsets[:], offs)
-        nc.sync.dma_start(pf_row[LAST:P, :], pf)
         nc.sync.dma_start(imp_win[LAST:P, :], imp[0:1, :])
+        nc.sync.dma_start(pf_row[LAST:P, :], pf)
+        nc.sync.dma_start(offsets[:], offs)
         key_rows = keys.rearrange("(p t) n -> t p n", t=PACK)
         key_planes = [sb.tile([P, T], F32, name=f"keys{t}", tag=f"keys{t}") for t in range(PACK)]
         wd_raw = sb.tile([P, PACK, M], F32, name="wd_raw")

@@ -24,8 +24,9 @@ PAGE = I // G
 LAST = P - 1
 GROUP = 16
 WEIGHT_PIECES = [128, 128, 256, 256, 256]
-VECTOR_SLOTS = {2: [320, 512], 3: [320, 608]}
-SCALAR_COLUMNS = (54, 72)
+HEAD = 256
+VECTOR_SLOTS = {2: [HEAD, 576], 3: [HEAD, 512]}
+SCALAR_COLUMNS = (48, 64)
 
 
 def tile_attend_pagesummary_pl_kernel(tc, keys, imp, pf, wd, offs, out_0, out_1, out_2):
@@ -41,7 +42,7 @@ def tile_attend_pagesummary_pl_kernel(tc, keys, imp, pf, wd, offs, out_0, out_1,
         nc.sync.dma_start(pf_row[LAST:P, :], pf)
         nc.sync.dma_start(offsets[:], offs)
         key_rows = keys.rearrange("(p t) n -> t p n", t=PACK)
-        key_planes = [sb.tile([P, T], F32, name=f"keys{t}", tag=f"keys{t}") for t in range(PACK)]
+        key_planes = [sb.tile([P, T], F32, name=f"keys{t}") for t in range(PACK)]
         wd_raw = sb.tile([P, PACK, M], F32, name="wd_raw")
         for t in range(PACK):
             nc.sync.dma_start(key_planes[t][:], key_rows[t])
@@ -56,7 +57,14 @@ def tile_attend_pagesummary_pl_kernel(tc, keys, imp, pf, wd, offs, out_0, out_1,
         def list_cols(first, count):
             return offsets[:, first // GROUP:(first + count) // GROUP]
 
-        weight = sb.tile([P, I], F32, name="weight")
+        weight_head = sb.tile([P, HEAD], F32, name="weight_head", tag="weight_head")
+        weight_rest = sb.tile([P, I - HEAD], F32, name="weight_rest")
+
+        def weight(first, count):
+            if first < HEAD:
+                return weight_head[:, first:first + count]
+            return weight_rest[:, first - HEAD:first - HEAD + count]
+
         starts = [sum(WEIGHT_PIECES[:q]) for q in range(len(WEIGHT_PIECES))]
         pf_slots = [sb.tile([P, n // PAGE, PAGE], F32, name=f"pf_slots{q}") for q, n in enumerate(WEIGHT_PIECES)]
         for q, (first, n) in enumerate(zip(starts, WEIGHT_PIECES)):
@@ -74,7 +82,7 @@ def tile_attend_pagesummary_pl_kernel(tc, keys, imp, pf, wd, offs, out_0, out_1,
                 nc.scalar.copy(weight_col[:], cols[:, LAST:P])
                 spread = ps.tile([P, P], F32, name=f"spread{block}", tag=f"bank{4 + block % 4}")
                 nc.tensor.transpose(spread[:], weight_col[:].to_broadcast([P, P]), ident[:])
-                nc.scalar.copy(weight[:, block * P:(block + 1) * P], spread[:])
+                nc.scalar.copy(weight(block * P, P), spread[:])
 
         first_grp = sb.tile([P, 3, P, PACK], BF16, name="first_grp", align_bytes=64)
         last_grp = sb.tile([P, 2, P, PACK], BF16, name="last_grp", align_bytes=64)
@@ -86,14 +94,14 @@ def tile_attend_pagesummary_pl_kernel(tc, keys, imp, pf, wd, offs, out_0, out_1,
             for h, count in enumerate(pieces):
                 first = sum(pieces[:h])
                 nc.vector.tensor_tensor(x[:, first:first + count], key_planes[t][:].indirect(list_cols(first, count)),
-                                        weight[:, first:first + count], MULT)
+                                        weight(first, count), MULT)
             return x[:].rearrange("p (g j) -> p g j", j=PAGE)
 
         def gather_rest(t, first):
             raw = sb.tile([P, I - first], F32, name=f"raw{t}")
             nc.scalar.activation(raw[:], key_planes[t][:].indirect(list_cols(first, I - first)), COPY)
             x_rest = sb.tile([P, I - first], F32, name=f"x_rest{t}")
-            nc.gpsimd.tensor_tensor(x_rest[:], raw[:], weight[:, first:I], MULT)
+            nc.gpsimd.tensor_tensor(x_rest[:], raw[:], weight(first, I - first), MULT)
             return x_rest[:].rearrange("p (g j) -> p g j", j=PAGE)
 
         def reduce_pages(t, first_page, x_pages):
@@ -101,14 +109,14 @@ def tile_attend_pagesummary_pl_kernel(tc, keys, imp, pf, wd, offs, out_0, out_1,
                 nc.vector.tensor_reduce(b_grp[:, first_page:first_page + x_pages.shape[1], t], x_pages, AXIS_X, ADD)
 
         sums = ps.tile([P, 2, P], F32, name="sums", tag="bank0")
-        for t, pieces in enumerate((WEIGHT_PIECES, [I])):
+        for t, pieces in enumerate((WEIGHT_PIECES, [HEAD, I - HEAD])):
             x_pages = gather(t, pieces)
             for j in range(PAGE):
                 nc.tensor.matmul(sums[:, t, :], x_pages[:, :, j], ident[:], start=(j == 0), stop=(j == PAGE - 1),
                                  is_transpose=True)
 
         def place_turned_sums():
-            pairs = sb.tile([P, P, 2], BF16, name="pairs", tag="keys2")
+            pairs = sb.tile([P, P, 2], BF16, name="pairs", tag="weight_head")
             nc.scalar.copy(pairs[:], sums[:].rearrange("g e p -> g p e"))
             back = ps.tile([P, G], F32, name="back", tag="bank7")
             nc.tensor.transpose(back[:], pairs[:].rearrange("g p e -> g (p e)").bitcast(F32), ident[:])
@@ -118,7 +126,7 @@ def tile_attend_pagesummary_pl_kernel(tc, keys, imp, pf, wd, offs, out_0, out_1,
         for t, pieces in VECTOR_SLOTS.items():
             x_pages = gather(t, pieces)
             rest_pages = gather_rest(t, sum(pieces))
-            if t == 2:
+            if t == 3:
                 place_turned_sums()
             cut = pieces[0] // PAGE
             reduce_pages(t, 0, x_pages[:, 0:cut, :])

@@ -25,8 +25,8 @@ LAST = P - 1
 GROUP = 16
 WEIGHT_PIECES = [128, 128, 256, 256, 256]
 HEAD = 256
-VECTOR_SLOTS = {2: [HEAD, 576], 3: [HEAD, 512]}
-SCALAR_COLUMNS = (48, 64)
+VECTOR_SLOTS = {2: [HEAD, 576], 3: [HEAD, 544]}
+SCALAR_COLUMNS = (44, 60)
 
 
 def tile_attend_pagesummary_pl_kernel(tc, keys, imp, pf, wd, offs, out_0, out_1, out_2):

@@ -26,7 +26,7 @@ GROUP = 16
 WEIGHT_PIECES = [128, 128, 256, 256, 256]
 HEAD = 256
 VECTOR_SLOTS = {2: [HEAD, 576], 3: [HEAD, 544]}
-SCALAR_COLUMNS = (44, 60)
+SCALAR_COLUMNS = (44, 56)
 
 
 def tile_attend_pagesummary_pl_kernel(tc, keys, imp, pf, wd, offs, out_0, out_1, out_2):

from contextlib import ExitStack

import concourse.mybir as mybir
from concourse.masks import make_identity

D, T, I, G, M = 512, 2048, 1024, 128, 512
FLOPS = 2 * D * M * G

F32 = mybir.dt.float32
BF16 = mybir.dt.bfloat16
U32 = mybir.dt.uint32
I32 = mybir.dt.int32
U16 = mybir.dt.uint16
U8 = mybir.dt.uint8
FP8X4 = mybir.dt.float8_e4m3fn_x4
MULT = mybir.AluOpType.mult
ADD = mybir.AluOpType.add
AXIS_X = mybir.AxisListType.X
COPY = mybir.ActivationFunctionType.Copy

P = 128
PACK = 4
PAGE = I // G
LAST = P - 1
GROUP = 16
WEIGHT_PIECES = [128, 128, 256, 256, 256]
HEAD = 256
VECTOR_SLOTS = {2: [HEAD, 576], 3: [HEAD, 544]}
SCALAR_COLUMNS = (44, 56)


def tile_attend_pagesummary_pl_kernel(tc, keys, imp, pf, wd, offs, out_0, out_1, out_2):
    nc = tc.nc
    with ExitStack() as ctx:
        sb = ctx.enter_context(tc.tile_pool(name="sb", bufs=1))
        ps = ctx.enter_context(tc.psum_pool(name="ps", bufs=1))

        offsets = sb.tile([P, I // GROUP], U16, name="offsets")
        imp_win = sb.tile([P, T], F32, name="imp_win")
        pf_row = sb.tile([P, G], F32, name="pf_row")
        nc.sync.dma_start(imp_win[LAST:P, :], imp[0:1, :])
        nc.sync.dma_start(pf_row[LAST:P, :], pf)
        nc.sync.dma_start(offsets[:], offs)
        key_rows = keys.rearrange("(p t) n -> t p n", t=PACK)
        key_planes = [sb.tile([P, T], F32, name=f"keys{t}") for t in range(PACK)]
        wd_raw = sb.tile([P, PACK, M], F32, name="wd_raw")
        for t in range(PACK):
            nc.sync.dma_start(key_planes[t][:], key_rows[t])
        nc.sync.dma_start(wd_raw[:], wd.rearrange("(p j) m -> p j m", j=PACK))

        nc.vector.memset(imp_win[0:LAST, 0:G], 0.0)
        nc.vector.memset(imp_win[0:LAST, G:T], 0.0)
        nc.scalar.copy(pf_row[0:LAST, :], imp_win[0:LAST, 0:G])
        ident = sb.tile([P, P], F32, name="ident")
        make_identity(nc, ident[:])

        def list_cols(first, count):
            return offsets[:, first // GROUP:(first + count) // GROUP]

        weight_head = sb.tile([P, HEAD], F32, name="weight_head", tag="weight_head")
        weight_rest = sb.tile([P, I - HEAD], F32, name="weight_rest")

        def weight(first, count):
            if first < HEAD:
                return weight_head[:, first:first + count]
            return weight_rest[:, first - HEAD:first - HEAD + count]

        starts = [sum(WEIGHT_PIECES[:q]) for q in range(len(WEIGHT_PIECES))]
        pf_slots = [sb.tile([P, n // PAGE, PAGE], F32, name=f"pf_slots{q}") for q, n in enumerate(WEIGHT_PIECES)]
        for q, (first, n) in enumerate(zip(starts, WEIGHT_PIECES)):
            pages = slice(first // PAGE, (first + n) // PAGE)
            nc.scalar.copy(pf_slots[q][:], pf_row[:, pages].unsqueeze(2).to_broadcast([P, n // PAGE, PAGE]))
        for q, (first, n) in enumerate(zip(starts, WEIGHT_PIECES)):
            weight_row = sb.tile([P, n], F32, name=f"weight_row{q}")
            nc.vector.tensor_tensor(weight_row[:], imp_win[:].indirect(list_cols(first, n)),
                                    pf_slots[q][:].rearrange("p g j -> p (g j)"), MULT)
            for c in range(n // P):
                block = first // P + c
                cols = ps.tile([P, P], F32, name=f"cols{block}", tag=f"bank{block % 4}")
                nc.tensor.transpose(cols[:], weight_row[:, c * P:(c + 1) * P], ident[:])
                weight_col = sb.tile([P, 1], F32, name=f"weight_col{block}")
                nc.scalar.copy(weight_col[:], cols[:, LAST:P])
                spread = ps.tile([P, P], F32, name=f"spread{block}", tag=f"bank{4 + block % 4}")
                nc.tensor.transpose(spread[:], weight_col[:].to_broadcast([P, P]), ident[:])
                nc.scalar.copy(weight(block * P, P), spread[:])

        first_grp = sb.tile([P, 3, P, PACK], BF16, name="first_grp", align_bytes=64)
        last_grp = sb.tile([P, 2, P, PACK], BF16, name="last_grp", align_bytes=64)
        b_grp = first_grp[:, 0]
        wd_pairs = (first_grp[:, 1:3], last_grp[:])

        def gather(t, pieces):
            x = sb.tile([P, sum(pieces)], F32, name=f"x{t}")
            for h, count in enumerate(pieces):
                first = sum(pieces[:h])
                nc.vector.tensor_tensor(x[:, first:first + count], key_planes[t][:].indirect(list_cols(first, count)),
                                        weight(first, count), MULT)
            return x[:].rearrange("p (g j) -> p g j", j=PAGE)

        def gather_rest(t, first):
            raw = sb.tile([P, I - first], F32, name=f"raw{t}")
            nc.scalar.activation(raw[:], key_planes[t][:].indirect(list_cols(first, I - first)), COPY)
            x_rest = sb.tile([P, I - first], F32, name=f"x_rest{t}")
            nc.gpsimd.tensor_tensor(x_rest[:], raw[:], weight(first, I - first), MULT)
            return x_rest[:].rearrange("p (g j) -> p g j", j=PAGE)

        def reduce_pages(t, first_page, x_pages):
            with nc.allow_low_precision(reason="float32 sum, rounded once on the way to the quantiser"):
                nc.vector.tensor_reduce(b_grp[:, first_page:first_page + x_pages.shape[1], t], x_pages, AXIS_X, ADD)

        sums = ps.tile([P, 2, P], F32, name="sums", tag="bank0")
        for t, pieces in enumerate((WEIGHT_PIECES, [HEAD, I - HEAD])):
            x_pages = gather(t, pieces)
            for j in range(PAGE):
                nc.tensor.matmul(sums[:, t, :], x_pages[:, :, j], ident[:], start=(j == 0), stop=(j == PAGE - 1),
                                 is_transpose=True)

        def place_turned_sums():
            pairs = sb.tile([P, P, 2], BF16, name="pairs", tag="weight_head")
            nc.scalar.copy(pairs[:], sums[:].rearrange("g e p -> g p e"))
            back = ps.tile([P, G], F32, name="back", tag="bank7")
            nc.tensor.transpose(back[:], pairs[:].rearrange("g p e -> g (p e)").bitcast(F32), ident[:])
            b_words = b_grp.rearrange("p g t -> p (g t)").bitcast(F32).rearrange("p (g u) -> p g u", u=2)
            nc.scalar.copy(b_words[:, :, 0], back[:])

        for t, pieces in VECTOR_SLOTS.items():
            x_pages = gather(t, pieces)
            rest_pages = gather_rest(t, sum(pieces))
            if t == 3:
                place_turned_sums()
            cut = pieces[0] // PAGE
            reduce_pages(t, 0, x_pages[:, 0:cut, :])
            reduce_pages(t, cut, x_pages[:, cut:sum(pieces) // PAGE, :])
            reduce_pages(t, sum(pieces) // PAGE, rest_pages)

        wd_dealt = wd_raw[:].rearrange("p j (s u e) -> p u s j e", u=2, e=2)
        for u, split in enumerate(SCALAR_COLUMNS):
            nc.vector.tensor_copy(wd_pairs[u][:, :, split:P, :].rearrange("p e s j -> p s j e"), wd_dealt[:, u, split:P])
        for u, split in enumerate(SCALAR_COLUMNS):
            nc.scalar.copy(wd_pairs[u][:, :, 0:split, :].rearrange("p e s j -> p s j e"), wd_dealt[:, u, 0:split])

        codes = sb.tile([P, 1 + PACK, P], U32, name="codes", align_bytes=64)
        scales = sb.tile([P, 1 + PACK, P], U8, name="scales", align_bytes=64)
        nc.vector.quantize_mx(out=codes[:, 0:2].rearrange("p a s -> p (a s)").bitcast(FP8X4),
                              scales=scales[:, 0:2].rearrange("p a s -> p (a s)"),
                              in_=first_grp[:, 0:2].rearrange("p a s j -> p (a s j)"))
        for t in range(1, PACK):
            nc.vector.quantize_mx(out=codes[:, 1 + t].bitcast(FP8X4), scales=scales[:, 1 + t],
                                  in_=wd_pairs[t // 2][:, t % 2].rearrange("p s j -> p (s j)"))

        halves = [slice(0, G // 2), slice(G // 2, G)]
        y = sb.tile([P, PACK, G], F32, name="y")
        for t in range(PACK):
            acc = ps.tile([P, G], F32, name=f"acc{t}", tag=f"bank{t}")
            nc.tensor.matmul_mx(out=acc[:], lhsT=codes[:, 1 + t].bitcast(FP8X4), lhsT_scale=scales[:, 1 + t],
                                rhs=codes[:, 0].bitcast(FP8X4), rhs_scale=scales[:, 0], start=True, stop=True)
            for pages in (halves if t == PACK - 1 else [slice(0, G)]):
                nc.scalar.copy(y[:, t, pages], acc[:, pages])
        nc.sync.dma_start(out_0.rearrange("(p t) g -> p t g", t=PACK), y[:])

        y_grp = sb.tile([P, G, PACK], BF16, name="y_grp", align_bytes=64)
        y_codes = sb.tile([P, G], U32, name="y_codes", align_bytes=64)
        y_scales = sb.tile([P, G], U8, name="y_scales", align_bytes=64)
        for pages, places in ((slice(0, G), slice(0, 2)), (halves[0], slice(2, 4)), (halves[1], slice(2, 4))):
            nc.vector.tensor_copy(y_grp[:, pages, places].rearrange("p (c i) t -> p c t i", i=4),
                                  y[:, places, pages].rearrange("p t (c i) -> p c t i", i=4))
        for pages in halves:
            nc.vector.quantize_mx(out=y_codes[:, pages].bitcast(FP8X4), scales=y_scales[:, pages],
                                  in_=y_grp[:, pages, :].rearrange("p g t -> p (g t)"))
        nc.sync.dma_start(out_1[0].rearrange("p c r -> p (c r)").bitcast(I32), y_codes[:].bitcast(I32))
        for q in range(4):
            queue = nc.sync if q < 2 else nc.scalar
            queue.dma_start(out_2[0, 4 * q:4 * q + 4, :].bitcast(I32), y_scales[32 * q:32 * q + 4, :].bitcast(I32))
